import numpy as np
import ml_dtypes


def mxq(x, axis, fmt="e4m3"):
    dtype, down = {"e4m3": (ml_dtypes.float8_e4m3fn, 7), "e5m2": (ml_dtypes.float8_e5m2, 14)}[fmt]
    v = np.moveaxis(np.asarray(x, np.float32).astype(ml_dtypes.bfloat16).astype(np.float64), axis, -1)
    blocks = v.reshape(v.shape[:-1] + (-1, 32))
    amax = np.abs(blocks).max(-1, keepdims=True)
    byte = np.maximum(np.where(amax > 0, np.frexp(amax)[1] - 1 + 127, 0) - down, 1)
    scale = np.exp2(byte - 127.0)
    codes = (blocks / scale).astype(np.float32).astype(dtype).astype(np.float64)
    return np.moveaxis((codes * scale).reshape(v.shape), -1, axis)


WIDE = False


def mx_kscale(k):
    if not WIDE:
        return np.ones(k)
    levels = np.array([10, -10, 5, -5, 0])
    if k % 512:
        return np.exp2(np.random.permutation(np.resize(levels, k // 32))).repeat(32)
    a = np.empty((k // 512, 16))
    for p in range(k // 512):
        a[p, :8] = np.random.permutation(np.resize(levels, 8))
        for g in range(8):
            far = levels[np.abs(levels - a[p, g]) >= 10]
            a[p, g + 8] = far[np.random.randint(len(far))]
    return np.exp2(a.ravel()).repeat(32)


BF16 = ml_dtypes.bfloat16


def bf(x):
    return np.asarray(x, np.float32).astype(BF16)


def f64(x):
    return np.asarray(x).astype(np.float64)


E2M1 = np.array([0.0, 0.5, 1.0, 1.5, 2.0, 3.0, 4.0, 6.0, -0.0, -0.5, -1.0, -1.5, -2.0, -3.0, -4.0, -6.0])


def pack_weight(w, fmt):
    k, n = w.shape
    w = f64(bf(w)).reshape(k // 32, 32, n)
    amax = np.abs(w).max(1)
    if fmt == "e4m3":
        byte = np.frexp(amax)[1] - 1 + 127 - 7
    else:
        mant, ex = np.frexp(amax / 6.0)
        byte = np.where(mant > 0.5, ex, ex - 1) + 127
    byte = np.clip(np.where(amax > 0, byte, 1), 1, 254)
    scaled = (w * np.exp2(127.0 - byte)[:, None, :]).reshape(k, n).astype(np.float32)
    by_word = np.ascontiguousarray(scaled.reshape(k // 512, 128, 4, n).transpose(0, 1, 3, 2))
    if fmt == "e4m3":
        words = by_word.astype(ml_dtypes.float8_e4m3fn).view(np.uint8)
    else:
        c = by_word.astype(ml_dtypes.float4_e2m1fn).view(np.uint8) & 0xF
        words = c[..., 0::2] | (c[..., 1::2] << 4)
    return np.ascontiguousarray(words), np.ascontiguousarray(byte.astype(np.uint8).reshape(k // 512, 16, n))


def unpack_weight(words, scales, fmt):
    g, p, n, _ = words.shape
    if fmt == "e4m3":
        vals = np.ascontiguousarray(words).view(ml_dtypes.float8_e4m3fn).astype(np.float64)
    else:
        nib = np.empty((g, p, n, 4), np.uint8)
        nib[..., 0::2] = words & 0xF
        nib[..., 1::2] = words >> 4
        vals = E2M1[nib]
    vals = vals * np.repeat(np.exp2(scales.astype(np.float64) - 127.0), 8, axis=1)[..., None]
    return vals.transpose(0, 1, 3, 2).reshape(g * 512, n)
def pack4(w):
    words, scales = pack_weight(w, "e2m1")
    return words.reshape(words.shape[0], 128, -1), scales


def unpack4(words, scales):
    return unpack_weight(words.reshape(words.shape[0], 128, -1, 2), scales, "e2m1")


B, S, D, M, N, C = 2, 1024, 512, 512, 512, 2


def cauchy_parts(om, nu, b):
    de = om[:, None] - nu[None, :]
    w = b[None, :] / (0.25 + de * de)
    gr = 0.5 * w
    gi = -de * w
    return gr, gi


def draw0():
    s, t, r = mx_kscale(S), mx_kscale(M), mx_kscale(N)
    x = bf(np.random.standard_normal((B, S, D)) / s[None, :, None])
    p = np.random.standard_normal((M, S)) / np.sqrt(S) * s[None, :] * t[:, None]
    p_words, p_scales = pack4(p.T)
    om = bf(np.random.uniform(-4.0, 4.0, M))
    nu = bf(np.random.uniform(-4.0, 4.0, N))
    b = bf(np.random.standard_normal(N) * r)
    c = np.random.standard_normal((N, D)) * 1.5 / np.sqrt(N) / r[:, None]
    c_words, c_scales = pack4(c)
    q = bf(np.random.standard_normal((C, S, M)) / np.sqrt(M) / t[None, None, :])
    return {"x": x,
            "p_words": p_words,
            "p_scales": p_scales,
            "om": om,
            "nu": nu,
            "b": b,
            "c_words": c_words,
            "c_scales": c_scales,
            "q": q}


def core(x, p_words, p_scales, om, nu, b, c_words, c_scales, q):
    gr, gi = cauchy_parts(f64(om), f64(nu), f64(b))
    gr, gi = gr, gi
    cq = unpack4(c_words, c_scales)
    kr = mxq(gr, 1, "e4m3") @ cq
    ki = mxq(gi, 1, "e4m3") @ cq
    u = unpack4(p_words, p_scales).T @ mxq(f64(x), 1, "e4m3")
    fr = kr[None, :, :] * u
    fi = ki[None, :, :] * u
    qq = mxq(f64(q), 2, "e4m3")
    return (qq[0] @ mxq(fr, 1, "e4m3")) - (qq[1] @ mxq(fi, 1, "e4m3"))


def e4m3fn_bytes(y):
    return np.clip(np.asarray(y, np.float64), -448.0, 448.0).astype(np.float32).astype(ml_dtypes.float8_e4m3fn).view(np.uint8)


def e4m3fn_values(b):
    return np.asarray(b, np.uint8).view(ml_dtypes.float8_e4m3fn).astype(np.float64)


def setup_inputs():
    d = draw0()
    x0 = np.asarray(d['x']).astype(np.float64)
    s = (np.max(np.abs(x0), axis=(0, 2), keepdims=True) / 448.0).astype(np.float32)
    out = {}
    for k, v in d.items():
        if k == 'x':
            out['x_bytes'] = e4m3fn_bytes(x0 / s.astype(np.float64))
            out['x_scale'] = s
        else:
            out[k] = v
    return out


def reference(x_bytes, x_scale, p_words, p_scales, om, nu, b, c_words, c_scales, q):
    return core(e4m3fn_values(x_bytes) * x_scale.astype(np.float64), p_words, p_scales, om, nu, b, c_words, c_scales, q)

@@ -1,0 +1,516 @@
+from contextlib import ExitStack
+
+import concourse.mybir as mybir
+from concourse.masks import make_identity
+
+B, S, D, M, N, C = 2, 1024, 512, 512, 512, 2
+FLOPS = 2 * (2 * M * N * D + B * M * S * D + 2 * B * S * M * D)
+
+F32 = mybir.dt.float32
+BF16 = mybir.dt.bfloat16
+U32 = mybir.dt.uint32
+I32 = mybir.dt.int32
+U8 = mybir.dt.uint8
+F8 = mybir.dt.float8_e4m3fn
+E4M3 = mybir.dt.float8_e4m3fn_x4
+E2M1 = mybir.dt.float4_e2m1fn_x4
+ALU = mybir.AluOpType
+ACT = mybir.ActivationFunctionType
+
+P = 128
+T = 4
+G = S // 512
+CH = D // P
+J = S // P
+UNITS = [[(0, 256), (256, 512)], [(0, 256), (256, 384), (384, 512)]]
+
+
+def tile_cauchytransferfunctionfilter_w4_kernel(
+    tc, x_bytes, x_scale, p_words, p_scales, om, nu, b, c_words, c_scales, q, out
+):
+    nc = tc.nc
+    with ExitStack() as ctx:
+        keep = ctx.enter_context(tc.tile_pool(name="keep", bufs=1))
+        outp = ctx.enter_context(tc.tile_pool(name="outp", bufs=6))
+        psum = ctx.enter_context(tc.psum_pool(name="psum", bufs=4))
+
+        lhs_rows = keep.tile([P, N], BF16)
+        rhs_rows = keep.tile([P, M], BF16)
+        quarter = keep.tile([P, 1], F32)
+        warm = keep.tile([P, 1], F32)
+        p_scale_raw = keep.tile([P, G, M], U8, align_bytes=64)
+        c_scale = keep.tile([P, D], U8, align_bytes=64)
+        nc.vector.memset(rhs_rows[:].bitcast(F32), 0.0)
+        nc.gpsimd.memset(lhs_rows[:].bitcast(F32), 0.0)
+        nc.vector.memset(quarter[:], 0.25)
+        nc.vector.memset(rhs_rows[32:33, :], -1.0)
+        nc.vector.memset(lhs_rows[0:1, :], 1.0)
+        nc.scalar.activation(out=warm[:], in_=quarter[:], func=ACT.Abs_reciprocal_sqrt, bias=quarter[:], scale=1.0)
+        nc.vector.memset(p_scale_raw[:].rearrange("p g m -> p (g m)").bitcast(I32), 0)
+        nc.vector.memset(c_scale[:].bitcast(I32), 0)
+        b_col = keep.tile([P, T], BF16)
+        xs = keep.tile([P, G, T], F32)
+        p_raw = keep.tile([P, G, 2 * M], U8, align_bytes=64)
+        c_raw = keep.tile([P, 2 * D], U8, align_bytes=64)
+        q_raw = keep.tile([P, C, J, M], BF16, align_bytes=64)
+        x_raw = {}
+
+        def load_vectors():
+            nc.sync.dma_start(out=rhs_rows[0:1, :], in_=om.rearrange("(o m) -> o m", o=1))
+            nc.sync.dma_start(out=lhs_rows[32:33, :], in_=nu.rearrange("(o n) -> o n", o=1))
+            nc.sync.dma_start(out=xs[:], in_=x_scale.rearrange("o (g p t) w -> p (o g) (t w)", p=P, t=T))
+            nc.sync.dma_start(out=b_col[:], in_=b.rearrange("(p t) -> p t", t=T))
+
+        for i in range(B):
+            for g in range(G):
+                x_raw_t = keep.tile([P, T * D], U8, name="x_raw_%d_%d" % (i, g))
+                x_raw[i, g] = x_raw_t
+
+        def load_x(i, g, t0, t1):
+            rows = x_bytes[i, g * 512 : (g + 1) * 512, :].rearrange("(p t) d -> p (t d)", t=T)
+            nc.sync.dma_start(out=x_raw[i, g][:, t0 * D : t1 * D], in_=rows[:, t0 * D : t1 * D])
+
+        def load_p():
+            nc.sync.dma_start(out=p_raw[:], in_=p_words.rearrange("g p w -> p g w"))
+
+        def load_p_scale():
+            for r4 in range(4):
+                nc.sync.dma_start(
+                    out=p_scale_raw[32 * r4 : 32 * r4 + 4, :, :].bitcast(I32),
+                    in_=p_scales[:, 4 * r4 : 4 * r4 + 4, :].rearrange("g q m -> q g m").bitcast(I32),
+                )
+
+        def load_c():
+            nc.sync.dma_start(out=c_raw[:], in_=c_words[0])
+
+        def load_c_scale():
+            for r4 in range(4):
+                nc.sync.dma_start(
+                    out=c_scale[32 * r4 : 32 * r4 + 4, :].bitcast(I32),
+                    in_=c_scales[0, 4 * r4 : 4 * r4 + 4, :].bitcast(I32),
+                )
+
+        def load_q(c, h):
+            nc.sync.dma_start(
+                out=q_raw[:, c, 4 * h : 4 * h + 4, :],
+                in_=q[c].rearrange("(p j) m -> p j m", j=J)[:, 4 * h : 4 * h + 4, :],
+            )
+
+        ident = keep.tile([P, P], F32)
+        make_identity(nc, ident[:])
+
+        ctx.enter_context(tc.manual_schedule())
+        r = keep.tile([P, T, M], F32)
+        w = keep.tile([P, T, M], F32)
+        de = {}
+
+        def make_de(tm):
+            de_ps = psum.tile([P, T, P], F32, tag="u")
+            de[tm] = de_ps
+            for t in range(T):
+                nc.tensor.matmul(
+                    out=de_ps[:, t, :], lhsT=lhs_rows[:, t::T], rhs=rhs_rows[:, tm::T], start=True, stop=True
+                )
+
+        def square(tm):
+            nc.scalar.activation(out=r[:, :, P * tm : P * (tm + 1)], in_=de[tm][:], func=ACT.Square)
+
+        def make_r(h):
+            cols = slice(256 * h, 256 * (h + 1))
+            nc.scalar.activation(
+                out=r[:, :, cols], in_=r[:, :, cols], func=ACT.Abs_reciprocal_sqrt, bias=quarter[:], scale=1.0
+            )
+
+        def make_w(h):
+            cols = slice(256 * h, 256 * (h + 1))
+            for t in range(T):
+                nc.vector.scalar_tensor_tensor(
+                    out=w[:, t, cols],
+                    in0=r[:, t, cols],
+                    scalar=b_col[:, t : t + 1],
+                    in1=r[:, t, cols],
+                    op0=ALU.mult,
+                    op1=ALU.mult,
+                )
+
+        g_bf, g_codes, g_scale = {}, {}, {}
+        for k in ("r", "i"):
+            g_bf_t = keep.tile([P, M, T], BF16, name="g_bf_" + k, align_bytes=64)
+            g_codes_t = keep.tile([P, M], U32, name="g_codes_" + k, align_bytes=64)
+            g_scale_t = keep.tile([P, M], U8, name="g_scale_" + k, align_bytes=64)
+            g_bf[k], g_codes[k], g_scale[k] = g_bf_t, g_codes_t, g_scale_t
+
+        w_mt = w[:].rearrange("p t m -> p m t")
+
+        def make_gr(h):
+            cols = slice(256 * h, 256 * (h + 1))
+            nc.gpsimd.tensor_scalar(
+                out=g_bf["r"][:, cols, :], in0=w_mt[:, cols, :], scalar1=0.5, scalar2=0.0, op0=ALU.mult, op1=ALU.add
+            )
+
+        def make_gi(tm):
+            sub = slice(P * tm, P * (tm + 1))
+            nc.vector.tensor_tensor(
+                out=g_bf["i"][:, sub, :],
+                in0=de[tm][:].rearrange("p t m -> p m t"),
+                in1=w_mt[:, sub, :],
+                op=ALU.mult,
+            )
+
+        def quant_g(k, h):
+            cols = slice(256 * h, 256 * (h + 1))
+            nc.vector.quantize_mx(
+                out=g_codes[k][:, cols].bitcast(E4M3),
+                scales=g_scale[k][:, cols],
+                in_=g_bf[k][:, cols, :].rearrange("p m t -> p (m t)"),
+            )
+
+        p_perm = keep.tile([P, G, 2 * M], U8, align_bytes=64)
+        p_scale = keep.tile([P, G, M], U8, align_bytes=64)
+
+        def make_p(g):
+            nc.vector.tensor_copy(
+                out=p_perm[:, g, :].rearrange("p (t m e) -> p t m e", t=T, e=2),
+                in_=p_raw[:, g, :].rearrange("p (m t e) -> p t m e", t=T, e=2),
+            )
+
+        def make_p_scale(g):
+            nc.vector.tensor_copy(
+                out=p_scale[:, g, :].rearrange("p (t m) -> p t m", t=T),
+                in_=p_scale_raw[:, g, :].rearrange("p (m t) -> p t m", t=T),
+            )
+
+        x_codes, x_sc = {}, {}
+
+        wide, inter = {}, {}
+
+        for i in range(B):
+            for g in range(G):
+                wide_t = keep.tile([P, T, D], BF16, name="wide_%d_%d" % (i, g), align_bytes=64)
+                wide[i, g] = wide_t
+
+        def widen_x(i, g, t, engine):
+            src = x_raw[i, g][:, t * D : (t + 1) * D].bitcast(F8)
+            scale = xs[:, g, t : t + 1]
+            dst = wide[i, g][:, t, :]
+            if engine == "v":
+                nc.vector.tensor_scalar(out=dst, in0=src, scalar1=scale, scalar2=None, op0=ALU.mult)
+            else:
+                nc.scalar.activation(out=dst, in_=src, func=ACT.Copy, scale=scale)
+
+        def drain(out_view, in_view, engine):
+            if engine == "v":
+                nc.vector.tensor_copy(out=out_view, in_=in_view)
+            else:
+                nc.scalar.copy(out=out_view, in_=in_view)
+
+        for i in range(B):
+            for g in range(G):
+                inter_t = keep.tile([P, D, T], BF16, name="inter_%d_%d" % (i, g), align_bytes=64)
+                inter[i, g] = inter_t
+
+        def inter_x(i, g, h):
+            cols = slice(256 * h, 256 * (h + 1))
+            nc.vector.tensor_copy(
+                out=inter[i, g][:, cols, :].rearrange("p (c e) t -> p c t e", e=4),
+                in_=wide[i, g][:, :, cols].rearrange("p t (c e) -> p c t e", e=4),
+            )
+
+        def quant_x(i, g):
+            x_codes_t = keep.tile([P, D], U32, name="x_codes_%d_%d" % (i, g), align_bytes=64)
+            x_sc_t = keep.tile([P, D], U8, name="x_sc_%d_%d" % (i, g), align_bytes=64)
+            nc.vector.quantize_mx(
+                out=x_codes_t[:].bitcast(E4M3), scales=x_sc_t[:], in_=inter[i, g][:].rearrange("p d t -> p (d t)")
+            )
+            x_codes[i, g], x_sc[i, g] = x_codes_t, x_sc_t
+
+        q_codes = keep.tile([P, C, S], U32, align_bytes=64)
+        q_sc = keep.tile([P, C, S], U8, align_bytes=64)
+        q_bf = keep.tile([P, C, S, T], BF16, align_bytes=64)
+
+        q_ps = {}
+
+        def turn_q(c, jj):
+            bank = psum.tile([P, 2, 2, P], F32, tag="a", name="q_ps")
+            q_ps[c, jj] = bank
+            words = q_raw[:, c, :, :].rearrange("p j m -> p (j m)").bitcast(F32)
+            for k in range(2):
+                for u in range(2):
+                    base = (2 * jj + k) * (M // 2)
+                    nc.tensor.transpose(bank[:, k, u, :], words[:, base + u : base + M // 2 : 2], ident[:])
+
+        def drain_q(c, jj, engine):
+            drain(
+                q_bf[:, c, 2 * jj * P : (2 * jj + 2) * P, :]
+                .rearrange("p s t -> p (s t)")
+                .bitcast(F32)
+                .rearrange("p (k s u) -> p k s u", k=2, u=2),
+                q_ps[c, jj][:].rearrange("p k u s -> p k s u"),
+                engine,
+            )
+
+        def quant_q(c, h):
+            rows = slice(h * 512, (h + 1) * 512)
+            nc.vector.quantize_mx(
+                out=q_codes[:, c, rows].bitcast(E4M3),
+                scales=q_sc[:, c, rows],
+                in_=q_bf[:, c, rows, :].rearrange("p s t -> p (s t)"),
+            )
+
+        k_sb = keep.tile([P, 2, CH, P, T], F32)
+        k_ps = {}
+
+        def make_k(k, ch):
+            bank = psum.tile([P, T, P], F32, tag="a", name="k_ps")
+            k_ps[k, ch] = bank
+            for t in range(T):
+                cols = slice(t * P, (t + 1) * P)
+                nc.tensor.matmul_mx(
+                    out=bank[:, t, :],
+                    lhsT=g_codes[k][:, cols].bitcast(E4M3),
+                    lhsT_scale=g_scale[k][:, cols],
+                    rhs=c_raw[:, 2 * P * ch : 2 * P * (ch + 1)].bitcast(E2M1),
+                    rhs_scale=c_scale[:, P * ch : P * (ch + 1)],
+                    start=True,
+                    stop=True,
+                )
+
+        def warm_pe(h):
+            bank = psum.tile([P, 512], F32, tag="a", name="warm_ps")
+            src = g_bf["r"][:].rearrange("p m t -> p (m t)")
+            for s in range(2):
+                cols = slice(1024 * h + 512 * s, 1024 * h + 512 * (s + 1))
+                nc.tensor.matmul(out=bank[:], lhsT=lhs_rows[:, 0:P], rhs=src[:, cols], start=True, stop=True)
+
+        def drain_k(k, ch, engine):
+            drain(k_sb[:, 0 if k == "r" else 1, ch, :, :], k_ps[k, ch][:].rearrange("p t d -> p d t"), engine)
+
+        f_bf, f_codes, f_sc = {}, {}, {}
+        for i in range(B):
+            for d0, d1 in UNITS[i]:
+                f_bf_t = keep.tile([P, 2, d1 - d0, T], BF16, name="f_bf_%d_%d" % (i, d0), align_bytes=64)
+                f_codes_t = keep.tile([P, 2, d1 - d0], U32, name="f_codes_%d_%d" % (i, d0), align_bytes=64)
+                f_sc_t = keep.tile([P, 2, d1 - d0], U8, name="f_sc_%d_%d" % (i, d0), align_bytes=64)
+                f_bf[i, d0], f_codes[i, d0], f_sc[i, d0] = f_bf_t, f_codes_t, f_sc_t
+        u_ps = {}
+
+        def make_u(i, ch):
+            bank = psum.tile([P, T, P], F32, tag="u", name="u_ps")
+            u_ps[i, ch] = bank
+            for t in range(T):
+                for g in range(G):
+                    nc.tensor.matmul_mx(
+                        out=bank[:, t, :],
+                        lhsT=p_perm[:, g, 2 * P * t : 2 * P * (t + 1)].bitcast(E2M1),
+                        lhsT_scale=p_scale[:, g, P * t : P * (t + 1)],
+                        rhs=x_codes[i, g][:, P * ch : P * (ch + 1)].bitcast(E4M3),
+                        rhs_scale=x_sc[i, g][:, P * ch : P * (ch + 1)],
+                        start=(g == 0),
+                        stop=(g == G - 1),
+                    )
+
+        def make_f(i, d0, ch):
+            nc.vector.tensor_tensor(
+                out=f_bf[i, d0][:, :, P * ch - d0 : P * (ch + 1) - d0, :],
+                in0=u_ps[i, ch][:].rearrange("p (o t) d -> p o d t", o=1).to_broadcast([P, 2, P, T]),
+                in1=k_sb[:, :, ch, :, :],
+                op=ALU.mult,
+            )
+
+        def quant_f(i, d0):
+            nc.vector.quantize_mx(
+                out=f_codes[i, d0][:].rearrange("p k d -> p (k d)").bitcast(E4M3),
+                scales=f_sc[i, d0][:].rearrange("p k d -> p (k d)"),
+                in_=f_bf[i, d0][:].rearrange("p k d t -> p (k d t)"),
+            )
+
+        o_ps = {}
+
+        def synth(i, d0, d1, jj):
+            width = d1 - d0
+            tiles = 512 // width
+            bank = psum.tile([P, tiles, width], F32, tag="a", name="o_ps")
+            for kk in range(tiles):
+                j = tiles * jj + kk
+                for c in range(C):
+                    cols = slice(j * P, (j + 1) * P)
+                    nc.tensor.matmul_mx(
+                        out=bank[:, kk, :],
+                        lhsT=q_codes[:, c, cols].bitcast(E4M3),
+                        lhsT_scale=q_sc[:, c, cols],
+                        rhs=f_codes[i, d0][:, c, :].bitcast(E4M3),
+                        rhs_scale=f_sc[i, d0][:, c, :],
+                        start=(c == 0),
+                        stop=(c == C - 1),
+                    )
+            o_ps[i, d0, jj] = bank
+
+        def store(i, d0, d1, jj, engine):
+            tiles = 512 // (d1 - d0)
+            bank = o_ps[i, d0, jj]
+            o_sb = outp.tile([P, 512], F32)
+            o_view = o_sb[:].rearrange("p (k d) -> p k d", k=tiles)
+            drain(o_view, bank[:], engine)
+            nc.sync.dma_start(
+                out=out[i].rearrange("(p j) d -> p j d", j=J)[:, tiles * jj : tiles * (jj + 1), d0:d1], in_=o_view
+            )
+
+        load_x(1, 1, 0, 4)
+        load_vectors()
+        make_de(0)
+        widen_x(1, 1, 1, "v")
+        make_de(1)
+        load_p()
+        load_x(0, 1, 0, 4)
+        widen_x(1, 1, 3, "s")
+        widen_x(1, 1, 0, "v")
+        make_de(2)
+        widen_x(1, 1, 2, "s")
+        load_q(0, 0)
+        make_p(0)
+        make_de(3)
+        widen_x(0, 1, 2, "s")
+        inter_x(1, 1, 0)
+        widen_x(0, 1, 3, "s")
+        widen_x(0, 1, 1, "s")
+        square(0)
+        load_q(1, 1)
+        square(1)
+        load_p_scale()
+        widen_x(0, 1, 0, "v")
+        square(3)
+        make_r(0)
+        make_p(1)
+        square(2)
+        inter_x(1, 1, 1)
+        inter_x(0, 1, 0)
+        load_x(0, 0, 2, 4)
+        turn_q(0, 0)
+        turn_q(1, 3)
+        drain_q(0, 0, "s")
+        load_x(0, 0, 0, 2)
+        inter_x(0, 1, 1)
+        drain_q(1, 3, "s")
+        quant_x(1, 1)
+        make_w(0)
+        turn_q(1, 2)
+        load_q(1, 0)
+        make_p_scale(0)
+        make_gr(0)
+        make_gi(0)
+        make_r(1)
+        drain_q(1, 2, "s")
+        make_gi(1)
+        turn_q(0, 1)
+        make_w(1)
+        turn_q(1, 0)
+        widen_x(0, 0, 3, "s")
+        quant_g("i", 0)
+        load_q(0, 1)
+        make_gi(2)
+        turn_q(0, 3)
+        drain_q(0, 1, "s")
+        widen_x(0, 0, 0, "s")
+        widen_x(0, 0, 1, "s")
+        drain_q(1, 0, "s")
+        turn_q(1, 1)
+        widen_x(0, 0, 2, "s")
+        turn_q(0, 2)
+        drain_q(0, 3, "s")
+        load_x(1, 0, 0, 4)
+        drain_q(1, 1, "s")
+        make_gi(3)
+        make_gr(1)
+        warm_pe(0)
+        drain_q(0, 2, "s")
+        widen_x(1, 0, 2, "s")
+        quant_g("r", 0)
+        load_c()
+        widen_x(1, 0, 1, "s")
+        quant_g("i", 1)
+        widen_x(1, 0, 0, "s")
+        widen_x(1, 0, 3, "s")
+        warm_pe(1)
+        quant_g("r", 1)
+        inter_x(0, 0, 1)
+        load_c_scale()
+        make_k("i", 1)
+        drain_k("i", 1, "s")
+        inter_x(0, 0, 0)
+        make_k("r", 0)
+        make_p_scale(1)
+        quant_x(0, 0)
+        quant_x(0, 1)
+        make_k("i", 0)
+        drain_k("r", 0, "s")
+        make_k("r", 1)
+        make_u(0, 1)
+        quant_q(0, 1)
+        inter_x(1, 0, 0)
+        make_u(0, 0)
+        make_k("i", 2)
+        make_k("r", 3)
+        drain_k("i", 0, "s")
+        inter_x(1, 0, 1)
+        drain_k("r", 1, "s")
+        quant_q(0, 0)
+        quant_x(1, 0)
+        make_k("r", 2)
+        make_k("i", 3)
+        make_f(0, 0, 1)
+        make_u(1, 3)
+        make_u(1, 1)
+        make_f(0, 0, 0)
+        quant_q(1, 1)
+        drain_k("r", 3, "s")
+        make_u(0, 2)
+        quant_f(0, 0)
+        quant_q(1, 0)
+        make_u(1, 0)
+        drain_k("i", 3, "s")
+        drain_k("i", 2, "s")
+        synth(0, 0, 256, 2)
+        make_f(1, 384, 3)
+        drain_k("r", 2, "s")
+        make_f(1, 0, 0)
+        synth(0, 0, 256, 1)
+        quant_f(1, 384)
+        make_f(1, 0, 1)
+        quant_f(1, 0)
+        synth(0, 0, 256, 0)
+        store(0, 0, 256, 2, "s")
+        store(0, 0, 256, 0, "s")
+        store(0, 0, 256, 1, "s")
+        synth(0, 0, 256, 3)
+        make_u(0, 3)
+        synth(1, 384, 512, 0)
+        synth(1, 384, 512, 1)
+        store(0, 0, 256, 3, "s")
+        make_f(0, 256, 3)
+        make_f(0, 256, 2)
+        synth(1, 0, 256, 1)
+        synth(1, 0, 256, 2)
+        quant_f(0, 256)
+        store(1, 384, 512, 0, "s")
+        store(1, 384, 512, 1, "s")
+        synth(1, 0, 256, 0)
+        store(1, 0, 256, 1, "s")
+        synth(1, 0, 256, 3)
+        make_u(1, 2)
+        store(1, 0, 256, 2, "s")
+        synth(0, 256, 512, 3)
+        store(1, 0, 256, 0, "s")
+        store(1, 0, 256, 3, "s")
+        make_f(1, 256, 2)
+        store(0, 256, 512, 3, "s")
+        synth(0, 256, 512, 0)
+        quant_f(1, 256)
+        synth(0, 256, 512, 1)
+        store(0, 256, 512, 0, "s")
+        synth(0, 256, 512, 2)
+        store(0, 256, 512, 1, "s")
+        store(0, 256, 512, 2, "s")
+        synth(1, 256, 384, 0)
+        synth(1, 256, 384, 1)
+        store(1, 256, 384, 0, "s")
+        store(1, 256, 384, 1, "s")

@@ -19,10 +19,12 @@ ACT = mybir.ActivationFunctionType
 
 P = 128
 T = 4
-G = S // 512
-CH = D // P
+G = S // (P * T)
 J = S // P
-UNITS = [[(0, 256), (256, 512)], [(0, 256), (256, 384), (384, 512)]]
+H = 256
+UNITS = [(0, 0), (1, 0), (0, 1), (1, 1)]
+CHUNKS = [(i, 2 * h + k) for i, h in UNITS for k in range(2)]
+PIECES = [[n] for n in range(len(CHUNKS))]
 
 
 def tile_cauchytransferfunctionfilter_w4_kernel(
@@ -33,484 +35,382 @@ def tile_cauchytransferfunctionfilter_w4_kernel(
         keep = ctx.enter_context(tc.tile_pool(name="keep", bufs=1))
         outp = ctx.enter_context(tc.tile_pool(name="outp", bufs=6))
         psum = ctx.enter_context(tc.psum_pool(name="psum", bufs=4))
+        ctx.enter_context(tc.manual_schedule())
+
+        def tiles(name, keys, shape, dtype):
+            made = {}
+            for key in keys:
+                one = keep.tile(shape, dtype, name=name + "_" + "_".join(str(v) for v in key), align_bytes=64)
+                made[key] = one
+            return made
 
         lhs_rows = keep.tile([P, N], BF16)
         rhs_rows = keep.tile([P, M], BF16)
         quarter = keep.tile([P, 1], F32)
         warm = keep.tile([P, 1], F32)
-        p_scale_raw = keep.tile([P, G, M], U8, align_bytes=64)
-        c_scale = keep.tile([P, D], U8, align_bytes=64)
-        nc.vector.memset(rhs_rows[:].bitcast(F32), 0.0)
-        nc.gpsimd.memset(lhs_rows[:].bitcast(F32), 0.0)
-        nc.vector.memset(quarter[:], 0.25)
-        nc.vector.memset(rhs_rows[32:33, :], -1.0)
-        nc.vector.memset(lhs_rows[0:1, :], 1.0)
-        nc.scalar.activation(out=warm[:], in_=quarter[:], func=ACT.Abs_reciprocal_sqrt, bias=quarter[:], scale=1.0)
-        nc.vector.memset(p_scale_raw[:].rearrange("p g m -> p (g m)").bitcast(I32), 0)
-        nc.vector.memset(c_scale[:].bitcast(I32), 0)
+        ident = keep.tile([P, P], F32)
         b_col = keep.tile([P, T], BF16)
         xs = keep.tile([P, G, T], F32)
         p_raw = keep.tile([P, G, 2 * M], U8, align_bytes=64)
+        p_scale_raw = keep.tile([P, G, M], U8, align_bytes=64)
+        p_perm = keep.tile([P, G, 2 * M], U8, align_bytes=64)
+        p_scale = keep.tile([P, G, M], U8, align_bytes=64)
         c_raw = keep.tile([P, 2 * D], U8, align_bytes=64)
-        q_raw = keep.tile([P, C, J, M], BF16, align_bytes=64)
-        x_raw = {}
-
-        def load_vectors():
-            nc.sync.dma_start(out=rhs_rows[0:1, :], in_=om.rearrange("(o m) -> o m", o=1))
-            nc.sync.dma_start(out=lhs_rows[32:33, :], in_=nu.rearrange("(o n) -> o n", o=1))
-            nc.sync.dma_start(out=xs[:], in_=x_scale.rearrange("o (g p t) w -> p (o g) (t w)", p=P, t=T))
-            nc.sync.dma_start(out=b_col[:], in_=b.rearrange("(p t) -> p t", t=T))
-
-        for i in range(B):
-            for g in range(G):
-                x_raw_t = keep.tile([P, T * D], U8, name="x_raw_%d_%d" % (i, g))
-                x_raw[i, g] = x_raw_t
-
-        def load_x(i, g, t0, t1):
-            rows = x_bytes[i, g * 512 : (g + 1) * 512, :].rearrange("(p t) d -> p (t d)", t=T)
-            nc.sync.dma_start(out=x_raw[i, g][:, t0 * D : t1 * D], in_=rows[:, t0 * D : t1 * D])
-
-        def load_p():
-            nc.sync.dma_start(out=p_raw[:], in_=p_words.rearrange("g p w -> p g w"))
-
-        def load_p_scale():
-            for r4 in range(4):
-                nc.sync.dma_start(
-                    out=p_scale_raw[32 * r4 : 32 * r4 + 4, :, :].bitcast(I32),
-                    in_=p_scales[:, 4 * r4 : 4 * r4 + 4, :].rearrange("g q m -> q g m").bitcast(I32),
-                )
-
-        def load_c():
-            nc.sync.dma_start(out=c_raw[:], in_=c_words[0])
-
-        def load_c_scale():
-            for r4 in range(4):
-                nc.sync.dma_start(
-                    out=c_scale[32 * r4 : 32 * r4 + 4, :].bitcast(I32),
-                    in_=c_scales[0, 4 * r4 : 4 * r4 + 4, :].bitcast(I32),
-                )
-
-        def load_q(c, h):
-            nc.sync.dma_start(
-                out=q_raw[:, c, 4 * h : 4 * h + 4, :],
-                in_=q[c].rearrange("(p j) m -> p j m", j=J)[:, 4 * h : 4 * h + 4, :],
-            )
-
-        ident = keep.tile([P, P], F32)
-        make_identity(nc, ident[:])
-
-        ctx.enter_context(tc.manual_schedule())
-        r = keep.tile([P, T, M], F32)
+        c_scale = keep.tile([P, D], U8, align_bytes=64)
+        x_raw = tiles("x_raw", [(i, g) for i in range(B) for g in range(G)], [P, T * D], U8)
+        q_raw = tiles("q_raw", [(c, hs) for c in range(C) for hs in range(2)], [P, J // 2, M], BF16)
+        q_bf = tiles("q_bf", [(c, hs) for c in range(C) for hs in range(2)], [P, S // 2, T], BF16)
+        q_codes = keep.tile([P, C, S], U32, align_bytes=64)
+        q_sc = keep.tile([P, C, S], U8, align_bytes=64)
+        root = keep.tile([P, T, M], F32)
         w = keep.tile([P, T, M], F32)
-        de = {}
+        parts = [("r",), ("i",)]
+        g_bf = tiles("g_bf", parts, [P, M, T], BF16)
+        g_codes = tiles("g_codes", parts, [P, M], U32)
+        g_sc = tiles("g_sc", parts, [P, M], U8)
+        k_sb = tiles("k_sb", [(ch,) for ch in range(D // P)], [P, 2, P, T], F32)
+        wide = tiles("wide", UNITS, [P, G, T, H], BF16)
+        inter = tiles("inter", CHUNKS, [P, G, P, T], BF16)
+        x_codes = tiles("x_codes", CHUNKS, [P, G, P], U32)
+        x_sc = tiles("x_sc", CHUNKS, [P, G, P], U8)
+        f_bf, f_codes, f_sc = {}, {}, {}
+        for n, piece in enumerate(PIECES):
+            width = P * len(piece)
+            f_bf.update(tiles("f_bf", [(n,)], [P, 2, width, T], BF16))
+            f_codes.update(tiles("f_codes", [(n,)], [P, 2, width], U32))
+            f_sc.update(tiles("f_sc", [(n,)], [P, 2, width], U8))
+        de_ps, q_ps, k_ps, u_ps, o_ps = {}, {}, {}, {}, {}
+
+        def load_x(i, g):
+            rows = x_bytes[i, g * P * T : (g + 1) * P * T, :].rearrange("(p t) d -> p (t d)", t=T)
+            nc.sync.dma_start(out=x_raw[i, g][:], in_=rows)
+
+        def load_q(c, hs):
+            rows = q[c].rearrange("(p j) m -> p j m", j=J)[:, 4 * hs : 4 * hs + 4, :]
+            nc.sync.dma_start(out=q_raw[c, hs][:], in_=rows)
+
+        def load_p_scales():
+            for quad in range(4):
+                nc.sync.dma_start(
+                    out=p_scale_raw[32 * quad : 32 * quad + 4, :, :].bitcast(I32),
+                    in_=p_scales[:, 4 * quad : 4 * quad + 4, :].rearrange("g r m -> r g m").bitcast(I32),
+                )
+
+        def load_c_scales():
+            for quad in range(4):
+                nc.sync.dma_start(
+                    out=c_scale[32 * quad : 32 * quad + 4, :].bitcast(I32),
+                    in_=c_scales[0, 4 * quad : 4 * quad + 4, :].bitcast(I32),
+                )
 
         def make_de(tm):
-            de_ps = psum.tile([P, T, P], F32, tag="u")
-            de[tm] = de_ps
+            bank = psum.tile([P, T, P], F32, tag="u", name="de_ps")
+            de_ps[tm] = bank
             for t in range(T):
                 nc.tensor.matmul(
-                    out=de_ps[:, t, :], lhsT=lhs_rows[:, t::T], rhs=rhs_rows[:, tm::T], start=True, stop=True
+                    out=bank[:, t, :], lhsT=lhs_rows[:, t::T], rhs=rhs_rows[:, tm::T], start=True, stop=True
                 )
 
         def square(tm):
-            nc.scalar.activation(out=r[:, :, P * tm : P * (tm + 1)], in_=de[tm][:], func=ACT.Square)
+            nc.scalar.activation(out=root[:, :, P * tm : P * (tm + 1)], in_=de_ps[tm][:], func=ACT.Square)
 
-        def make_r(h):
-            cols = slice(256 * h, 256 * (h + 1))
+        def make_root(hm):
+            cols = slice(256 * hm, 256 * (hm + 1))
             nc.scalar.activation(
-                out=r[:, :, cols], in_=r[:, :, cols], func=ACT.Abs_reciprocal_sqrt, bias=quarter[:], scale=1.0
+                out=root[:, :, cols], in_=root[:, :, cols], func=ACT.Abs_reciprocal_sqrt, bias=quarter[:], scale=1.0
             )
 
-        def make_w(h):
-            cols = slice(256 * h, 256 * (h + 1))
+        def make_w(hm):
+            cols = slice(256 * hm, 256 * (hm + 1))
             for t in range(T):
                 nc.vector.scalar_tensor_tensor(
                     out=w[:, t, cols],
-                    in0=r[:, t, cols],
+                    in0=root[:, t, cols],
                     scalar=b_col[:, t : t + 1],
-                    in1=r[:, t, cols],
+                    in1=root[:, t, cols],
                     op0=ALU.mult,
                     op1=ALU.mult,
                 )
 
-        g_bf, g_codes, g_scale = {}, {}, {}
-        for k in ("r", "i"):
-            g_bf_t = keep.tile([P, M, T], BF16, name="g_bf_" + k, align_bytes=64)
-            g_codes_t = keep.tile([P, M], U32, name="g_codes_" + k, align_bytes=64)
-            g_scale_t = keep.tile([P, M], U8, name="g_scale_" + k, align_bytes=64)
-            g_bf[k], g_codes[k], g_scale[k] = g_bf_t, g_codes_t, g_scale_t
-
         w_mt = w[:].rearrange("p t m -> p m t")
 
-        def make_gr(h):
-            cols = slice(256 * h, 256 * (h + 1))
-            nc.gpsimd.tensor_scalar(
-                out=g_bf["r"][:, cols, :], in0=w_mt[:, cols, :], scalar1=0.5, scalar2=0.0, op0=ALU.mult, op1=ALU.add
-            )
+        def make_gr(hm, engine):
+            cols = slice(256 * hm, 256 * (hm + 1))
+            dst, src = g_bf["r",][:, cols, :], w_mt[:, cols, :]
+            if engine == "scalar":
+                nc.scalar.activation(out=dst, in_=src, func=ACT.Copy, scale=0.5)
+            else:
+                nc.gpsimd.tensor_scalar(out=dst, in0=src, scalar1=0.5, scalar2=0.0, op0=ALU.mult, op1=ALU.add)
 
         def make_gi(tm):
-            sub = slice(P * tm, P * (tm + 1))
+            cols = slice(P * tm, P * (tm + 1))
             nc.vector.tensor_tensor(
-                out=g_bf["i"][:, sub, :],
-                in0=de[tm][:].rearrange("p t m -> p m t"),
-                in1=w_mt[:, sub, :],
+                out=g_bf["i",][:, cols, :],
+                in0=de_ps[tm][:].rearrange("p t m -> p m t"),
+                in1=w_mt[:, cols, :],
                 op=ALU.mult,
             )
 
-        def quant_g(k, h):
-            cols = slice(256 * h, 256 * (h + 1))
+        def quant_g(part):
             nc.vector.quantize_mx(
-                out=g_codes[k][:, cols].bitcast(E4M3),
-                scales=g_scale[k][:, cols],
-                in_=g_bf[k][:, cols, :].rearrange("p m t -> p (m t)"),
+                out=g_codes[part,][:].bitcast(E4M3),
+                scales=g_sc[part,][:],
+                in_=g_bf[part,][:].rearrange("p m t -> p (m t)"),
             )
 
-        p_perm = keep.tile([P, G, 2 * M], U8, align_bytes=64)
-        p_scale = keep.tile([P, G, M], U8, align_bytes=64)
-
-        def make_p(g):
+        def permute_p():
             nc.vector.tensor_copy(
-                out=p_perm[:, g, :].rearrange("p (t m e) -> p t m e", t=T, e=2),
-                in_=p_raw[:, g, :].rearrange("p (m t e) -> p t m e", t=T, e=2),
+                out=p_perm[:].rearrange("p g (t m e) -> p g t m e", t=T, e=2),
+                in_=p_raw[:].rearrange("p g (m t e) -> p g t m e", t=T, e=2),
             )
 
-        def make_p_scale(g):
+        def permute_p_scales():
             nc.vector.tensor_copy(
-                out=p_scale[:, g, :].rearrange("p (t m) -> p t m", t=T),
-                in_=p_scale_raw[:, g, :].rearrange("p (m t) -> p t m", t=T),
+                out=p_scale[:].rearrange("p g (t m) -> p g t m", t=T),
+                in_=p_scale_raw[:].rearrange("p g (m t) -> p g t m", t=T),
             )
 
-        x_codes, x_sc = {}, {}
+        def widen_x(unit, g, engine):
+            i, h = unit
+            for t in range(T):
+                src = x_raw[i, g][:, t * D + h * H : t * D + (h + 1) * H].bitcast(F8)
+                scale = xs[:, g, t : t + 1]
+                dst = wide[unit][:, g, t, :]
+                if engine == "vector":
+                    nc.vector.tensor_scalar(out=dst, in0=src, scalar1=scale, scalar2=None, op0=ALU.mult)
+                else:
+                    nc.scalar.activation(out=dst, in_=src, func=ACT.Copy, scale=scale)
 
-        wide, inter = {}, {}
+        def interleave_x(n, engine):
+            i, ch = CHUNKS[n]
+            cols = slice(P * (ch % 2), P * (ch % 2 + 1))
+            drain(
+                inter[i, ch][:].rearrange("p g (c e) t -> p g c t e", e=4),
+                wide[i, ch // 2][:, :, :, cols].rearrange("p g t (c e) -> p g c t e", e=4),
+                engine,
+            )
 
-        for i in range(B):
-            for g in range(G):
-                wide_t = keep.tile([P, T, D], BF16, name="wide_%d_%d" % (i, g), align_bytes=64)
-                wide[i, g] = wide_t
-
-        def widen_x(i, g, t, engine):
-            src = x_raw[i, g][:, t * D : (t + 1) * D].bitcast(F8)
-            scale = xs[:, g, t : t + 1]
-            dst = wide[i, g][:, t, :]
-            if engine == "v":
-                nc.vector.tensor_scalar(out=dst, in0=src, scalar1=scale, scalar2=None, op0=ALU.mult)
-            else:
-                nc.scalar.activation(out=dst, in_=src, func=ACT.Copy, scale=scale)
+        def quant_x(n):
+            chunk = CHUNKS[n]
+            nc.vector.quantize_mx(
+                out=x_codes[chunk][:].rearrange("p g d -> p (g d)").bitcast(E4M3),
+                scales=x_sc[chunk][:].rearrange("p g d -> p (g d)"),
+                in_=inter[chunk][:].rearrange("p g d t -> p (g d t)"),
+            )
 
         def drain(out_view, in_view, engine):
-            if engine == "v":
+            if engine == "vector":
                 nc.vector.tensor_copy(out=out_view, in_=in_view)
             else:
                 nc.scalar.copy(out=out_view, in_=in_view)
 
-        for i in range(B):
-            for g in range(G):
-                inter_t = keep.tile([P, D, T], BF16, name="inter_%d_%d" % (i, g), align_bytes=64)
-                inter[i, g] = inter_t
-
-        def inter_x(i, g, h):
-            cols = slice(256 * h, 256 * (h + 1))
-            nc.vector.tensor_copy(
-                out=inter[i, g][:, cols, :].rearrange("p (c e) t -> p c t e", e=4),
-                in_=wide[i, g][:, :, cols].rearrange("p t (c e) -> p c t e", e=4),
-            )
-
-        def quant_x(i, g):
-            x_codes_t = keep.tile([P, D], U32, name="x_codes_%d_%d" % (i, g), align_bytes=64)
-            x_sc_t = keep.tile([P, D], U8, name="x_sc_%d_%d" % (i, g), align_bytes=64)
-            nc.vector.quantize_mx(
-                out=x_codes_t[:].bitcast(E4M3), scales=x_sc_t[:], in_=inter[i, g][:].rearrange("p d t -> p (d t)")
-            )
-            x_codes[i, g], x_sc[i, g] = x_codes_t, x_sc_t
-
-        q_codes = keep.tile([P, C, S], U32, align_bytes=64)
-        q_sc = keep.tile([P, C, S], U8, align_bytes=64)
-        q_bf = keep.tile([P, C, S, T], BF16, align_bytes=64)
-
-        q_ps = {}
-
-        def turn_q(c, jj):
+        def turn_q(c, hs, jj):
             bank = psum.tile([P, 2, 2, P], F32, tag="a", name="q_ps")
-            q_ps[c, jj] = bank
-            words = q_raw[:, c, :, :].rearrange("p j m -> p (j m)").bitcast(F32)
+            q_ps[c, hs, jj] = bank
+            words = q_raw[c, hs][:].rearrange("p j m -> p (j m)").bitcast(F32)
             for k in range(2):
+                base = (2 * jj + k) * (M // 2)
                 for u in range(2):
-                    base = (2 * jj + k) * (M // 2)
                     nc.tensor.transpose(bank[:, k, u, :], words[:, base + u : base + M // 2 : 2], ident[:])
 
-        def drain_q(c, jj, engine):
+        def drain_q(c, hs, jj, engine):
             drain(
-                q_bf[:, c, 2 * jj * P : (2 * jj + 2) * P, :]
+                q_bf[c, hs][:, 2 * jj * P : (2 * jj + 2) * P, :]
                 .rearrange("p s t -> p (s t)")
                 .bitcast(F32)
                 .rearrange("p (k s u) -> p k s u", k=2, u=2),
-                q_ps[c, jj][:].rearrange("p k u s -> p k s u"),
+                q_ps[c, hs, jj][:].rearrange("p k u s -> p k s u"),
                 engine,
             )
 
-        def quant_q(c, h):
-            rows = slice(h * 512, (h + 1) * 512)
+        def quant_q(c, hs):
+            rows = slice(hs * S // 2, (hs + 1) * S // 2)
             nc.vector.quantize_mx(
                 out=q_codes[:, c, rows].bitcast(E4M3),
                 scales=q_sc[:, c, rows],
-                in_=q_bf[:, c, rows, :].rearrange("p s t -> p (s t)"),
+                in_=q_bf[c, hs][:].rearrange("p s t -> p (s t)"),
             )
 
-        k_sb = keep.tile([P, 2, CH, P, T], F32)
-        k_ps = {}
-
-        def make_k(k, ch):
+        def make_k(part, ch):
             bank = psum.tile([P, T, P], F32, tag="a", name="k_ps")
-            k_ps[k, ch] = bank
+            k_ps[part, ch] = bank
             for t in range(T):
                 cols = slice(t * P, (t + 1) * P)
                 nc.tensor.matmul_mx(
                     out=bank[:, t, :],
-                    lhsT=g_codes[k][:, cols].bitcast(E4M3),
-                    lhsT_scale=g_scale[k][:, cols],
+                    lhsT=g_codes[part,][:, cols].bitcast(E4M3),
+                    lhsT_scale=g_sc[part,][:, cols],
                     rhs=c_raw[:, 2 * P * ch : 2 * P * (ch + 1)].bitcast(E2M1),
                     rhs_scale=c_scale[:, P * ch : P * (ch + 1)],
                     start=True,
                     stop=True,
                 )
 
-        def warm_pe(h):
-            bank = psum.tile([P, 512], F32, tag="a", name="warm_ps")
-            src = g_bf["r"][:].rearrange("p m t -> p (m t)")
-            for s in range(2):
-                cols = slice(1024 * h + 512 * s, 1024 * h + 512 * (s + 1))
-                nc.tensor.matmul(out=bank[:], lhsT=lhs_rows[:, 0:P], rhs=src[:, cols], start=True, stop=True)
+        def drain_k(part, ch):
+            nc.scalar.copy(out=k_sb[ch,][:, "ri".index(part), :, :], in_=k_ps[part, ch][:].rearrange("p t d -> p d t"))
 
-        def drain_k(k, ch, engine):
-            drain(k_sb[:, 0 if k == "r" else 1, ch, :, :], k_ps[k, ch][:].rearrange("p t d -> p d t"), engine)
+        def transfer(ch):
+            for part in "ir":
+                make_k(part, ch)
+                drain_k(part, ch)
 
-        f_bf, f_codes, f_sc = {}, {}, {}
-        for i in range(B):
-            for d0, d1 in UNITS[i]:
-                f_bf_t = keep.tile([P, 2, d1 - d0, T], BF16, name="f_bf_%d_%d" % (i, d0), align_bytes=64)
-                f_codes_t = keep.tile([P, 2, d1 - d0], U32, name="f_codes_%d_%d" % (i, d0), align_bytes=64)
-                f_sc_t = keep.tile([P, 2, d1 - d0], U8, name="f_sc_%d_%d" % (i, d0), align_bytes=64)
-                f_bf[i, d0], f_codes[i, d0], f_sc[i, d0] = f_bf_t, f_codes_t, f_sc_t
-        u_ps = {}
-
-        def make_u(i, ch):
+        def make_u(n):
+            chunk = CHUNKS[n]
             bank = psum.tile([P, T, P], F32, tag="u", name="u_ps")
-            u_ps[i, ch] = bank
+            u_ps[n] = bank
             for t in range(T):
                 for g in range(G):
                     nc.tensor.matmul_mx(
                         out=bank[:, t, :],
                         lhsT=p_perm[:, g, 2 * P * t : 2 * P * (t + 1)].bitcast(E2M1),
                         lhsT_scale=p_scale[:, g, P * t : P * (t + 1)],
-                        rhs=x_codes[i, g][:, P * ch : P * (ch + 1)].bitcast(E4M3),
-                        rhs_scale=x_sc[i, g][:, P * ch : P * (ch + 1)],
+                        rhs=x_codes[chunk][:, g, :].bitcast(E4M3),
+                        rhs_scale=x_sc[chunk][:, g, :],
                         start=(g == 0),
                         stop=(g == G - 1),
                     )
 
-        def make_f(i, d0, ch):
+        piece_of = {n: (k, piece.index(n)) for k, piece in enumerate(PIECES) for n in piece}
+
+        def make_f(n):
+            k, place = piece_of[n]
             nc.vector.tensor_tensor(
-                out=f_bf[i, d0][:, :, P * ch - d0 : P * (ch + 1) - d0, :],
-                in0=u_ps[i, ch][:].rearrange("p (o t) d -> p o d t", o=1).to_broadcast([P, 2, P, T]),
-                in1=k_sb[:, :, ch, :, :],
+                out=f_bf[k,][:, :, P * place : P * (place + 1), :],
+                in0=u_ps[n][:].rearrange("p (o t) d -> p o d t", o=1).to_broadcast([P, 2, P, T]),
+                in1=k_sb[CHUNKS[n][1],][:],
                 op=ALU.mult,
             )
 
-        def quant_f(i, d0):
+        def quant_f(n):
             nc.vector.quantize_mx(
-                out=f_codes[i, d0][:].rearrange("p k d -> p (k d)").bitcast(E4M3),
-                scales=f_sc[i, d0][:].rearrange("p k d -> p (k d)"),
-                in_=f_bf[i, d0][:].rearrange("p k d t -> p (k d t)"),
+                out=f_codes[n,][:].rearrange("p k d -> p (k d)").bitcast(E4M3),
+                scales=f_sc[n,][:].rearrange("p k d -> p (k d)"),
+                in_=f_bf[n,][:].rearrange("p k d t -> p (k d t)"),
             )
 
-        o_ps = {}
-
-        def synth(i, d0, d1, jj):
-            width = d1 - d0
-            tiles = 512 // width
-            bank = psum.tile([P, tiles, width], F32, tag="a", name="o_ps")
-            for kk in range(tiles):
-                j = tiles * jj + kk
+        def synth(n, jj):
+            width = P * len(PIECES[n])
+            count = 512 // width
+            bank = psum.tile([P, count, width], F32, tag="a", name="o_ps")
+            o_ps[n, jj] = bank
+            for k in range(count):
+                cols = slice((count * jj + k) * P, (count * jj + k + 1) * P)
                 for c in range(C):
-                    cols = slice(j * P, (j + 1) * P)
                     nc.tensor.matmul_mx(
-                        out=bank[:, kk, :],
+                        out=bank[:, k, :],
                         lhsT=q_codes[:, c, cols].bitcast(E4M3),
                         lhsT_scale=q_sc[:, c, cols],
-                        rhs=f_codes[i, d0][:, c, :].bitcast(E4M3),
-                        rhs_scale=f_sc[i, d0][:, c, :],
+                        rhs=f_codes[n,][:, c, :].bitcast(E4M3),
+                        rhs_scale=f_sc[n,][:, c, :],
                         start=(c == 0),
                         stop=(c == C - 1),
                     )
-            o_ps[i, d0, jj] = bank
 
-        def store(i, d0, d1, jj, engine):
-            tiles = 512 // (d1 - d0)
-            bank = o_ps[i, d0, jj]
+        def store(n, jj, engine):
+            i, ch = CHUNKS[PIECES[n][0]]
+            width = P * len(PIECES[n])
+            count = 512 // width
             o_sb = outp.tile([P, 512], F32)
-            o_view = o_sb[:].rearrange("p (k d) -> p k d", k=tiles)
-            drain(o_view, bank[:], engine)
-            nc.sync.dma_start(
-                out=out[i].rearrange("(p j) d -> p j d", j=J)[:, tiles * jj : tiles * (jj + 1), d0:d1], in_=o_view
-            )
+            o_view = o_sb[:].rearrange("p (k d) -> p k d", k=count)
+            drain(o_view, o_ps[n, jj][:], engine)
+            d0 = ch * P
+            rows = out[i].rearrange("(p j) d -> p j d", j=J)[:, count * jj : count * (jj + 1), d0 : d0 + width]
+            nc.sync.dma_start(out=rows, in_=o_view)
 
-        load_x(1, 1, 0, 4)
-        load_vectors()
-        make_de(0)
-        widen_x(1, 1, 1, "v")
-        make_de(1)
-        load_p()
-        load_x(0, 1, 0, 4)
-        widen_x(1, 1, 3, "s")
-        widen_x(1, 1, 0, "v")
-        make_de(2)
-        widen_x(1, 1, 2, "s")
+        def synth_store(n, last_engine="scalar"):
+            banks = J * P * len(PIECES[n]) // 512
+            for jj in range(banks):
+                synth(n, jj)
+                store(n, jj, last_engine if jj == banks - 1 else "scalar")
+
+        nc.sync.dma_start(out=rhs_rows[31:32, :], in_=om.rearrange("(o m) -> o m", o=1))
+        nc.sync.dma_start(out=lhs_rows[63:64, :], in_=nu.rearrange("(o n) -> o n", o=1))
+        nc.sync.dma_start(out=xs[:], in_=x_scale.rearrange("o (g p t) w -> p (o g) (t w)", p=P, t=T))
+        load_x(0, 0)
+        load_x(0, 1)
+        nc.sync.dma_start(out=p_raw[:], in_=p_words.rearrange("g p w -> p g w"))
+        nc.sync.dma_start(out=b_col[:], in_=b.rearrange("(p t) -> p t", t=T))
         load_q(0, 0)
-        make_p(0)
-        make_de(3)
-        widen_x(0, 1, 2, "s")
-        inter_x(1, 1, 0)
-        widen_x(0, 1, 3, "s")
-        widen_x(0, 1, 1, "s")
-        square(0)
-        load_q(1, 1)
-        square(1)
-        load_p_scale()
-        widen_x(0, 1, 0, "v")
-        square(3)
-        make_r(0)
-        make_p(1)
-        square(2)
-        inter_x(1, 1, 1)
-        inter_x(0, 1, 0)
-        load_x(0, 0, 2, 4)
-        turn_q(0, 0)
-        turn_q(1, 3)
-        drain_q(0, 0, "s")
-        load_x(0, 0, 0, 2)
-        inter_x(0, 1, 1)
-        drain_q(1, 3, "s")
-        quant_x(1, 1)
-        make_w(0)
-        turn_q(1, 2)
+
+        make_identity(nc, ident[:])
+        nc.vector.memset(quarter[:], 0.25)
+        nc.scalar.activation(out=warm[:], in_=quarter[:], func=ACT.Abs_reciprocal_sqrt, bias=quarter[:], scale=1.0)
+        nc.vector.memset(lhs_rows[0:32, :], 1.0)
+        nc.vector.memset(rhs_rows[32:64, :], -1.0)
+        nc.vector.memset(rhs_rows[0:31, :].bitcast(F32), 0.0)
+        nc.vector.memset(lhs_rows[32:63, :].bitcast(F32), 0.0)
+        nc.vector.memset(rhs_rows[64:128, :].bitcast(F32), 0.0)
+        nc.vector.memset(lhs_rows[64:128, :].bitcast(F32), 0.0)
+        nc.vector.memset(p_scale_raw[:].rearrange("p g m -> p (g m)").bitcast(I32), 0)
+        nc.vector.memset(c_scale[:].bitcast(I32), 0)
+
+        load_p_scales()
         load_q(1, 0)
-        make_p_scale(0)
-        make_gr(0)
-        make_gi(0)
-        make_r(1)
-        drain_q(1, 2, "s")
-        make_gi(1)
-        turn_q(0, 1)
-        make_w(1)
-        turn_q(1, 0)
-        widen_x(0, 0, 3, "s")
-        quant_g("i", 0)
         load_q(0, 1)
-        make_gi(2)
-        turn_q(0, 3)
-        drain_q(0, 1, "s")
-        widen_x(0, 0, 0, "s")
-        widen_x(0, 0, 1, "s")
-        drain_q(1, 0, "s")
-        turn_q(1, 1)
-        widen_x(0, 0, 2, "s")
-        turn_q(0, 2)
-        drain_q(0, 3, "s")
-        load_x(1, 0, 0, 4)
-        drain_q(1, 1, "s")
-        make_gi(3)
-        make_gr(1)
-        warm_pe(0)
-        drain_q(0, 2, "s")
-        widen_x(1, 0, 2, "s")
-        quant_g("r", 0)
-        load_c()
-        widen_x(1, 0, 1, "s")
-        quant_g("i", 1)
-        widen_x(1, 0, 0, "s")
-        widen_x(1, 0, 3, "s")
-        warm_pe(1)
-        quant_g("r", 1)
-        inter_x(0, 0, 1)
-        load_c_scale()
-        make_k("i", 1)
-        drain_k("i", 1, "s")
-        inter_x(0, 0, 0)
-        make_k("r", 0)
-        make_p_scale(1)
-        quant_x(0, 0)
-        quant_x(0, 1)
-        make_k("i", 0)
-        drain_k("r", 0, "s")
-        make_k("r", 1)
-        make_u(0, 1)
-        quant_q(0, 1)
-        inter_x(1, 0, 0)
-        make_u(0, 0)
-        make_k("i", 2)
-        make_k("r", 3)
-        drain_k("i", 0, "s")
-        inter_x(1, 0, 1)
-        drain_k("r", 1, "s")
-        quant_q(0, 0)
-        quant_x(1, 0)
-        make_k("r", 2)
-        make_k("i", 3)
-        make_f(0, 0, 1)
-        make_u(1, 3)
-        make_u(1, 1)
-        make_f(0, 0, 0)
-        quant_q(1, 1)
-        drain_k("r", 3, "s")
-        make_u(0, 2)
-        quant_f(0, 0)
-        quant_q(1, 0)
-        make_u(1, 0)
-        drain_k("i", 3, "s")
-        drain_k("i", 2, "s")
-        synth(0, 0, 256, 2)
-        make_f(1, 384, 3)
-        drain_k("r", 2, "s")
-        make_f(1, 0, 0)
-        synth(0, 0, 256, 1)
-        quant_f(1, 384)
-        make_f(1, 0, 1)
-        quant_f(1, 0)
-        synth(0, 0, 256, 0)
-        store(0, 0, 256, 2, "s")
-        store(0, 0, 256, 0, "s")
-        store(0, 0, 256, 1, "s")
-        synth(0, 0, 256, 3)
-        make_u(0, 3)
-        synth(1, 384, 512, 0)
-        synth(1, 384, 512, 1)
-        store(0, 0, 256, 3, "s")
-        make_f(0, 256, 3)
-        make_f(0, 256, 2)
-        synth(1, 0, 256, 1)
-        synth(1, 0, 256, 2)
-        quant_f(0, 256)
-        store(1, 384, 512, 0, "s")
-        store(1, 384, 512, 1, "s")
-        synth(1, 0, 256, 0)
-        store(1, 0, 256, 1, "s")
-        synth(1, 0, 256, 3)
-        make_u(1, 2)
-        store(1, 0, 256, 2, "s")
-        synth(0, 256, 512, 3)
-        store(1, 0, 256, 0, "s")
-        store(1, 0, 256, 3, "s")
-        make_f(1, 256, 2)
-        store(0, 256, 512, 3, "s")
-        synth(0, 256, 512, 0)
-        quant_f(1, 256)
-        synth(0, 256, 512, 1)
-        store(0, 256, 512, 0, "s")
-        synth(0, 256, 512, 2)
-        store(0, 256, 512, 1, "s")
-        store(0, 256, 512, 2, "s")
-        synth(1, 256, 384, 0)
-        synth(1, 256, 384, 1)
-        store(1, 256, 384, 0, "s")
-        store(1, 256, 384, 1, "s")
+        load_q(1, 1)
+        nc.sync.dma_start(out=c_raw[:], in_=c_words[0])
+        load_c_scales()
+        load_x(1, 0)
+        load_x(1, 1)
+
+        q_banks = [(c, hs, jj) for hs in range(2) for c in range(C) for jj in range(2)]
+        for tm in range(T):
+            make_de(tm)
+        for bank in q_banks[:4]:
+            turn_q(*bank)
+        for tm in range(3):
+            square(tm)
+        make_root(0)
+        square(3)
+        drain_q(*q_banks[0], "scalar")
+        make_root(1)
+        for g in range(G):
+            widen_x(UNITS[0], g, "vector")
+        permute_p()
+        interleave_x(0, "vector")
+        make_w(0)
+        for bank in q_banks[1:4]:
+            drain_q(*bank, "scalar")
+        make_gr(0, "scalar")
+        for bank in q_banks[4:]:
+            turn_q(*bank)
+            drain_q(*bank, "scalar")
+        interleave_x(1, "vector")
+        permute_p_scales()
+        make_w(1)
+        quant_x(0)
+        make_gr(1, "gpsimd")
+        for tm in range(T):
+            make_gi(tm)
+        quant_x(1)
+        make_u(0)
+        make_u(1)
+        for g in range(G):
+            widen_x(UNITS[1], g, "scalar")
+        quant_g("i")
+        quant_g("r")
+        transfer(0)
+        transfer(1)
+        for hs in range(2):
+            for c in range(C):
+                quant_q(c, hs)
+        for g in range(G):
+            widen_x(UNITS[2], g, "scalar")
+        transfer(2)
+
+        for n in range(len(CHUNKS)):
+            ahead = n + 2
+            if ahead < len(CHUNKS):
+                interleave_x(ahead, "vector")
+            make_f(n)
+            if ahead < len(CHUNKS):
+                quant_x(ahead)
+                make_u(ahead)
+            k, place = piece_of[n]
+            if place == len(PIECES[k]) - 1:
+                quant_f(k)
+                synth_store(k, "vector" if k == len(PIECES) - 1 else "scalar")
+            if n < G:
+                widen_x(UNITS[3], n, "scalar")
+            if n == 2:
+                transfer(3)

@@ -10,6 +10,7 @@ F32 = mybir.dt.float32
 BF16 = mybir.dt.bfloat16
 U32 = mybir.dt.uint32
 I32 = mybir.dt.int32
+U16 = mybir.dt.uint16
 U8 = mybir.dt.uint8
 F8 = mybir.dt.float8_e4m3fn
 E4M3 = mybir.dt.float8_e4m3fn_x4
@@ -33,7 +34,8 @@ def tile_cauchytransferfunctionfilter_w4_kernel(
     nc = tc.nc
     with ExitStack() as ctx:
         keep = ctx.enter_context(tc.tile_pool(name="keep", bufs=1))
-        outp = ctx.enter_context(tc.tile_pool(name="outp", bufs=6))
+        stage = ctx.enter_context(tc.tile_pool(name="stage", bufs=1))
+        outp = ctx.enter_context(tc.tile_pool(name="outp", bufs=8))
         psum = ctx.enter_context(tc.psum_pool(name="psum", bufs=4))
         ctx.enter_context(tc.manual_schedule())
 
@@ -70,15 +72,15 @@ def tile_cauchytransferfunctionfilter_w4_kernel(
         g_sc = tiles("g_sc", parts, [P, M], U8)
         k_sb = tiles("k_sb", [(ch,) for ch in range(D // P)], [P, 2, P, T], F32)
         wide = tiles("wide", UNITS, [P, G, T, H], BF16)
-        inter = tiles("inter", CHUNKS, [P, G, P, T], BF16)
+        inter = {}
         x_codes = tiles("x_codes", CHUNKS, [P, G, P], U32)
         x_sc = tiles("x_sc", CHUNKS, [P, G, P], U8)
         f_bf, f_codes, f_sc = {}, {}, {}
-        for n, piece in enumerate(PIECES):
+        for k, piece in enumerate(PIECES):
             width = P * len(piece)
-            f_bf.update(tiles("f_bf", [(n,)], [P, 2, width, T], BF16))
-            f_codes.update(tiles("f_codes", [(n,)], [P, 2, width], U32))
-            f_sc.update(tiles("f_sc", [(n,)], [P, 2, width], U8))
+            f_bf.update(tiles("f_bf", [(k,)], [P, 2, width, T], BF16))
+            f_codes.update(tiles("f_codes", [(k,)], [P, 2, width], U32))
+            f_sc.update(tiles("f_sc", [(k,)], [P, 2, width], U8))
         de_ps, q_ps, k_ps, u_ps, o_ps = {}, {}, {}, {}, {}
 
         def load_x(i, g):
@@ -132,22 +134,27 @@ def tile_cauchytransferfunctionfilter_w4_kernel(
                     op1=ALU.mult,
                 )
 
-        w_mt = w[:].rearrange("p t m -> p m t")
+        def in_runs(planes):
+            return planes.rearrange("p t (c e) -> p c t e", e=4)
 
-        def make_gr(hm, engine):
-            cols = slice(256 * hm, 256 * (hm + 1))
-            dst, src = g_bf["r",][:, cols, :], w_mt[:, cols, :]
+        def out_runs(words):
+            return words.rearrange("p (c e) t -> p c t e", e=4)
+
+        def make_gr(tm, engine):
+            cols = slice(P * tm, P * (tm + 1))
+            dst, src = g_bf["r",][:, cols, :], w[:, :, cols]
             if engine == "scalar":
-                nc.scalar.activation(out=dst, in_=src, func=ACT.Copy, scale=0.5)
+                nc.scalar.activation(out=out_runs(dst), in_=in_runs(src), func=ACT.Copy, scale=0.5)
             else:
+                src = src.rearrange("p t m -> p m t")
                 nc.gpsimd.tensor_scalar(out=dst, in0=src, scalar1=0.5, scalar2=0.0, op0=ALU.mult, op1=ALU.add)
 
         def make_gi(tm):
             cols = slice(P * tm, P * (tm + 1))
             nc.vector.tensor_tensor(
-                out=g_bf["i",][:, cols, :],
-                in0=de_ps[tm][:].rearrange("p t m -> p m t"),
-                in1=w_mt[:, cols, :],
+                out=out_runs(g_bf["i",][:, cols, :]),
+                in0=in_runs(de_ps[tm][:]),
+                in1=in_runs(w[:, :, cols]),
                 op=ALU.mult,
             )
 
@@ -160,8 +167,8 @@ def tile_cauchytransferfunctionfilter_w4_kernel(
 
         def permute_p():
             nc.vector.tensor_copy(
-                out=p_perm[:].rearrange("p g (t m e) -> p g t m e", t=T, e=2),
-                in_=p_raw[:].rearrange("p g (m t e) -> p g t m e", t=T, e=2),
+                out=p_perm[:].bitcast(U16).rearrange("p g (t m) -> p g t m", t=T),
+                in_=p_raw[:].bitcast(U16).rearrange("p g (m t) -> p g t m", t=T),
             )
 
         def permute_p_scales():
@@ -181,22 +188,40 @@ def tile_cauchytransferfunctionfilter_w4_kernel(
                 else:
                     nc.scalar.activation(out=dst, in_=src, func=ACT.Copy, scale=scale)
 
-        def interleave_x(n, engine):
+        def chunk_planes(n):
             i, ch = CHUNKS[n]
-            cols = slice(P * (ch % 2), P * (ch % 2 + 1))
-            drain(
-                inter[i, ch][:].rearrange("p g (c e) t -> p g c t e", e=4),
-                wide[i, ch // 2][:, :, :, cols].rearrange("p g t (c e) -> p g c t e", e=4),
-                engine,
+            return wide[i, ch // 2][:, :, :, P * (ch % 2) : P * (ch % 2 + 1)]
+
+        def interleave_x(n):
+            dst = keep.tile([P, G, P, T], BF16, name="inter_%d" % n, align_bytes=64)
+            inter[n] = [(slice(0, G), dst[:].rearrange("p g d t -> p (g d t)"))]
+            nc.vector.tensor_copy(
+                out=dst[:].rearrange("p g (c e) t -> p g c t e", e=4),
+                in_=chunk_planes(n).rearrange("p g t (c e) -> p g c t e", e=4),
             )
+
+        def interleave_pass(n, g, engine):
+            src = chunk_planes(n)[:, g, :, :]
+            if g == 0:
+                dst = keep.tile([P, P, T], BF16, name="inter_%d" % n, align_bytes=64)
+            else:
+                dst = stage.tile([P, P, T], BF16, tag="inter_second", name="inter", align_bytes=64)
+            inter.setdefault(n, []).append((slice(g, g + 1), dst[:].rearrange("p d t -> p (d t)")))
+            if engine == "gpsimd":
+                nc.gpsimd.tensor_scalar(
+                    out=dst[:], in0=src.rearrange("p t d -> p d t"), scalar1=1.0, scalar2=0.0, op0=ALU.mult, op1=ALU.add
+                )
+            else:
+                nc.vector.tensor_copy(out=out_runs(dst[:]), in_=in_runs(src))
 
         def quant_x(n):
             chunk = CHUNKS[n]
-            nc.vector.quantize_mx(
-                out=x_codes[chunk][:].rearrange("p g d -> p (g d)").bitcast(E4M3),
-                scales=x_sc[chunk][:].rearrange("p g d -> p (g d)"),
-                in_=inter[chunk][:].rearrange("p g d t -> p (g d t)"),
-            )
+            for passes, words in inter[n]:
+                nc.vector.quantize_mx(
+                    out=x_codes[chunk][:, passes, :].rearrange("p g d -> p (g d)").bitcast(E4M3),
+                    scales=x_sc[chunk][:, passes, :].rearrange("p g d -> p (g d)"),
+                    in_=words,
+                )
 
         def drain(out_view, in_view, engine):
             if engine == "vector":
@@ -281,50 +306,56 @@ def tile_cauchytransferfunctionfilter_w4_kernel(
                 op=ALU.mult,
             )
 
-        def quant_f(n):
+        def quant_f(k):
             nc.vector.quantize_mx(
-                out=f_codes[n,][:].rearrange("p k d -> p (k d)").bitcast(E4M3),
-                scales=f_sc[n,][:].rearrange("p k d -> p (k d)"),
-                in_=f_bf[n,][:].rearrange("p k d t -> p (k d t)"),
+                out=f_codes[k,][:].rearrange("p k d -> p (k d)").bitcast(E4M3),
+                scales=f_sc[k,][:].rearrange("p k d -> p (k d)"),
+                in_=f_bf[k,][:].rearrange("p k d t -> p (k d t)"),
             )
 
-        def synth(n, jj):
-            width = P * len(PIECES[n])
-            count = 512 // width
-            bank = psum.tile([P, count, width], F32, tag="a", name="o_ps")
-            o_ps[n, jj] = bank
-            for k in range(count):
-                cols = slice((count * jj + k) * P, (count * jj + k + 1) * P)
+        def synth(k, jj, count, tag="a"):
+            bank = psum.tile([P, count, P * len(PIECES[k])], F32, tag=tag, name="o_ps")
+            o_ps[k, jj] = bank
+            for r in range(count):
+                cols = slice((count * jj + r) * P, (count * jj + r + 1) * P)
                 for c in range(C):
                     nc.tensor.matmul_mx(
-                        out=bank[:, k, :],
+                        out=bank[:, r, :],
                         lhsT=q_codes[:, c, cols].bitcast(E4M3),
                         lhsT_scale=q_sc[:, c, cols],
-                        rhs=f_codes[n,][:, c, :].bitcast(E4M3),
-                        rhs_scale=f_sc[n,][:, c, :],
+                        rhs=f_codes[k,][:, c, :].bitcast(E4M3),
+                        rhs_scale=f_sc[k,][:, c, :],
                         start=(c == 0),
                         stop=(c == C - 1),
                     )
 
-        def store(n, jj, engine):
-            i, ch = CHUNKS[PIECES[n][0]]
-            width = P * len(PIECES[n])
-            count = 512 // width
-            o_sb = outp.tile([P, 512], F32)
-            o_view = o_sb[:].rearrange("p (k d) -> p k d", k=count)
-            drain(o_view, o_ps[n, jj][:], engine)
-            d0 = ch * P
-            rows = out[i].rearrange("(p j) d -> p j d", j=J)[:, count * jj : count * (jj + 1), d0 : d0 + width]
-            nc.sync.dma_start(out=rows, in_=o_view)
+        def store(k, jj, engine="scalar"):
+            i, ch = CHUNKS[PIECES[k][0]]
+            bank = o_ps[k, jj]
+            count, width = bank.shape[1], bank.shape[2]
+            o_sb = outp.tile([P, count, width], F32)
+            drain(o_sb[:], bank[:], engine)
+            rows = out[i].rearrange("(p j) d -> p j d", j=J)[:, count * jj : count * (jj + 1), ch * P : ch * P + width]
+            nc.sync.dma_start(out=rows, in_=o_sb[:])
 
-        def synth_store(n, last_engine="scalar"):
-            banks = J * P * len(PIECES[n]) // 512
-            for jj in range(banks):
-                synth(n, jj)
-                store(n, jj, last_engine if jj == banks - 1 else "scalar")
+        def synth_chunk(k):
+            for jj in range(2):
+                synth(k, jj, 4)
 
-        nc.sync.dma_start(out=rhs_rows[31:32, :], in_=om.rearrange("(o m) -> o m", o=1))
-        nc.sync.dma_start(out=lhs_rows[63:64, :], in_=nu.rearrange("(o n) -> o n", o=1))
+        def store_chunk(k):
+            for jj in range(2):
+                store(k, jj)
+
+        def make_transfer(ch):
+            for part in "ir":
+                make_k(part, ch)
+
+        def drain_transfer(ch):
+            for part in "ir":
+                drain_k(part, ch)
+
+        nc.scalar.dma_start(out=rhs_rows[31:32, :], in_=om.rearrange("(o m) -> o m", o=1))
+        nc.scalar.dma_start(out=lhs_rows[63:64, :], in_=nu.rearrange("(o n) -> o n", o=1))
         nc.sync.dma_start(out=xs[:], in_=x_scale.rearrange("o (g p t) w -> p (o g) (t w)", p=P, t=T))
         load_x(0, 0)
         load_x(0, 1)
@@ -346,12 +377,12 @@ def tile_cauchytransferfunctionfilter_w4_kernel(
 
         load_p_scales()
         load_q(1, 0)
-        load_q(0, 1)
-        load_q(1, 1)
-        nc.sync.dma_start(out=c_raw[:], in_=c_words[0])
-        load_c_scales()
         load_x(1, 0)
         load_x(1, 1)
+        load_q(0, 1)
+        nc.sync.dma_start(out=c_raw[:], in_=c_words[0])
+        load_c_scales()
+        load_q(1, 1)
 
         q_banks = [(c, hs, jj) for hs in range(2) for c in range(C) for jj in range(2)]
         for tm in range(T):
@@ -367,50 +398,79 @@ def tile_cauchytransferfunctionfilter_w4_kernel(
         for g in range(G):
             widen_x(UNITS[0], g, "vector")
         permute_p()
-        interleave_x(0, "vector")
+        interleave_x(0)
+        permute_p_scales()
+        interleave_x(1)
         make_w(0)
+        quant_x(0)
+        make_gr(0, "gpsimd")
+        make_gi(0)
+        make_gi(1)
         for bank in q_banks[1:4]:
             drain_q(*bank, "scalar")
-        make_gr(0, "scalar")
-        for bank in q_banks[4:]:
+        make_gr(1, "scalar")
+        make_w(1)
+        quant_x(1)
+        make_gr(2, "gpsimd")
+        make_gi(2)
+        make_gi(3)
+        widen_x(UNITS[1], 0, "scalar")
+        make_gr(3, "scalar")
+        widen_x(UNITS[1], 1, "scalar")
+        for bank in q_banks[4:6]:
             turn_q(*bank)
             drain_q(*bank, "scalar")
-        interleave_x(1, "vector")
-        permute_p_scales()
-        make_w(1)
-        quant_x(0)
-        make_gr(1, "gpsimd")
-        for tm in range(T):
-            make_gi(tm)
-        quant_x(1)
         make_u(0)
         make_u(1)
-        for g in range(G):
-            widen_x(UNITS[1], g, "scalar")
+        quant_q(0, 0)
         quant_g("i")
         quant_g("r")
         transfer(0)
+        for bank in q_banks[6:]:
+            turn_q(*bank)
+            drain_q(*bank, "scalar")
         transfer(1)
-        for hs in range(2):
-            for c in range(C):
-                quant_q(c, hs)
-        for g in range(G):
-            widen_x(UNITS[2], g, "scalar")
-        transfer(2)
+        interleave_x(2)
+        interleave_x(3)
+        quant_x(2)
+        make_u(2)
+        quant_x(3)
+        make_u(3)
+        quant_q(1, 0)
+        make_transfer(2)
+        widen_x(UNITS[2], 0, "scalar")
 
-        for n in range(len(CHUNKS)):
-            ahead = n + 2
-            if ahead < len(CHUNKS):
-                interleave_x(ahead, "vector")
-            make_f(n)
-            if ahead < len(CHUNKS):
-                quant_x(ahead)
-                make_u(ahead)
-            k, place = piece_of[n]
-            if place == len(PIECES[k]) - 1:
-                quant_f(k)
-                synth_store(k, "vector" if k == len(PIECES) - 1 else "scalar")
-            if n < G:
-                widen_x(UNITS[3], n, "scalar")
-            if n == 2:
+        last = len(CHUNKS) - 1
+        make_f(0)
+        quant_q(0, 1)
+        quant_f(0)
+        quant_q(1, 1)
+        drain_transfer(2)
+        synth_chunk(0)
+        store_chunk(0)
+        widen_x(UNITS[2], 1, "vector")
+        make_f(1)
+        for n in range(2, last):
+            if n in (2, 3):
+                widen_x(UNITS[3], (2, 3).index(n), "scalar")
+            if n > 2:
+                store_chunk(n - 2)
+            if n == 3:
                 transfer(3)
+            if n + 2 <= last:
+                interleave_x(n + 2)
+            quant_f(n - 1)
+            synth_chunk(n - 1)
+            make_f(n)
+            if n + 2 <= last:
+                quant_x(n + 2)
+                make_u(n + 2)
+        store_chunk(last - 2)
+        quant_f(last - 1)
+        synth_chunk(last - 1)
+        store_chunk(last - 1)
+        make_f(last)
+        quant_f(last)
+        for jj in range(4):
+            synth(last, jj, 2, "uuaa"[jj])
+            store(last, jj, "vector" if jj % 2 else "scalar")

@@ -177,9 +177,9 @@ def tile_cauchytransferfunctionfilter_w4_kernel(
                 in_=p_scale_raw[:].rearrange("p g (m t) -> p g t m", t=T),
             )
 
-        def widen_x(unit, g, engine):
+        def widen_x(unit, g, engine, slots=range(T)):
             i, h = unit
-            for t in range(T):
+            for t in slots:
                 src = x_raw[i, g][:, t * D + h * H : t * D + (h + 1) * H].bitcast(F8)
                 scale = xs[:, g, t : t + 1]
                 dst = wide[unit][:, g, t, :]
@@ -354,8 +354,8 @@ def tile_cauchytransferfunctionfilter_w4_kernel(
             for part in "ir":
                 drain_k(part, ch)
 
-        nc.scalar.dma_start(out=rhs_rows[31:32, :], in_=om.rearrange("(o m) -> o m", o=1))
-        nc.scalar.dma_start(out=lhs_rows[63:64, :], in_=nu.rearrange("(o n) -> o n", o=1))
+        nc.sync.dma_start(out=rhs_rows[31:32, :], in_=om.rearrange("(o m) -> o m", o=1))
+        nc.sync.dma_start(out=lhs_rows[63:64, :], in_=nu.rearrange("(o n) -> o n", o=1))
         nc.sync.dma_start(out=xs[:], in_=x_scale.rearrange("o (g p t) w -> p (o g) (t w)", p=P, t=T))
         load_x(0, 0)
         load_x(0, 1)
@@ -393,24 +393,24 @@ def tile_cauchytransferfunctionfilter_w4_kernel(
             square(tm)
         make_root(0)
         square(3)
-        drain_q(*q_banks[0], "scalar")
+        widen_x(UNITS[2], 0, "scalar", range(1))
         make_root(1)
         for g in range(G):
             widen_x(UNITS[0], g, "vector")
         permute_p()
         interleave_x(0)
-        permute_p_scales()
         interleave_x(1)
-        make_w(0)
         quant_x(0)
+        make_w(0)
+        quant_x(1)
         make_gr(0, "gpsimd")
         make_gi(0)
         make_gi(1)
-        for bank in q_banks[1:4]:
+        for bank in q_banks[:4]:
             drain_q(*bank, "scalar")
         make_gr(1, "scalar")
         make_w(1)
-        quant_x(1)
+        permute_p_scales()
         make_gr(2, "gpsimd")
         make_gi(2)
         make_gi(3)
@@ -430,21 +430,21 @@ def tile_cauchytransferfunctionfilter_w4_kernel(
             turn_q(*bank)
             drain_q(*bank, "scalar")
         transfer(1)
+        quant_q(1, 0)
         interleave_x(2)
         interleave_x(3)
         quant_x(2)
         make_u(2)
         quant_x(3)
         make_u(3)
-        quant_q(1, 0)
         make_transfer(2)
-        widen_x(UNITS[2], 0, "scalar")
+        widen_x(UNITS[2], 0, "scalar", range(1, T))
 
         last = len(CHUNKS) - 1
-        make_f(0)
         quant_q(0, 1)
-        quant_f(0)
+        make_f(0)
         quant_q(1, 1)
+        quant_f(0)
         drain_transfer(2)
         synth_chunk(0)
         store_chunk(0)

@@ -78,7 +78,8 @@ def tile_cauchytransferfunctionfilter_w4_kernel(
         f_bf, f_codes, f_sc = {}, {}, {}
         for k, piece in enumerate(PIECES):
             width = P * len(piece)
-            f_bf.update(tiles("f_bf", [(k,)], [P, 2, width, T], BF16))
+            f_words = stage.tile([P, 2, width, T], BF16, tag="f_%d" % k, name="f_bf", align_bytes=64)
+            f_bf[k,] = f_words
             f_codes.update(tiles("f_codes", [(k,)], [P, 2, width], U32))
             f_sc.update(tiles("f_sc", [(k,)], [P, 2, width], U8))
         de_ps, q_ps, k_ps, u_ps, o_ps = {}, {}, {}, {}, {}
@@ -205,7 +206,7 @@ def tile_cauchytransferfunctionfilter_w4_kernel(
             if g == 0:
                 dst = keep.tile([P, P, T], BF16, name="inter_%d" % n, align_bytes=64)
             else:
-                dst = stage.tile([P, P, T], BF16, tag="inter_second", name="inter", align_bytes=64)
+                dst = stage.tile([P, P, T], BF16, tag="f_%d" % (n - 3), name="inter", align_bytes=64)
             inter.setdefault(n, []).append((slice(g, g + 1), dst[:].rearrange("p d t -> p (d t)")))
             if engine == "gpsimd":
                 nc.gpsimd.tensor_scalar(
@@ -448,19 +449,20 @@ def tile_cauchytransferfunctionfilter_w4_kernel(
         drain_transfer(2)
         synth_chunk(0)
         store_chunk(0)
-        widen_x(UNITS[2], 1, "vector")
         make_f(1)
+        widen_x(UNITS[2], 1, "vector")
         for n in range(2, last):
             if n in (2, 3):
-                widen_x(UNITS[3], (2, 3).index(n), "scalar")
+                widen_x(UNITS[3], n - 2, "scalar")
             if n > 2:
                 store_chunk(n - 2)
             if n == 3:
                 transfer(3)
-            if n + 2 <= last:
-                interleave_x(n + 2)
             quant_f(n - 1)
             synth_chunk(n - 1)
+            if n + 2 <= last:
+                interleave_pass(n + 2, 0, "vector")
+                interleave_pass(n + 2, 1, "gpsimd")
             make_f(n)
             if n + 2 <= last:
                 quant_x(n + 2)

@@ -452,10 +452,10 @@ def tile_cauchytransferfunctionfilter_w4_kernel(
         make_f(1)
         widen_x(UNITS[2], 1, "vector")
         for n in range(2, last):
-            if n in (2, 3):
-                widen_x(UNITS[3], n - 2, "scalar")
             if n > 2:
                 store_chunk(n - 2)
+            if n in (2, 3):
+                widen_x(UNITS[3], n - 2, "scalar")
             if n == 3:
                 transfer(3)
             quant_f(n - 1)

@@ -258,7 +258,7 @@ def tile_cauchytransferfunctionfilter_w4_kernel(
             )
 
         def make_k(part, ch):
-            bank = psum.tile([P, T, P], F32, tag="a", name="k_ps")
+            bank = psum.tile([P, T, P], F32, tag="u" if ch == D // P - 1 else "a", name="k_ps")
             k_ps[part, ch] = bank
             for t in range(T):
                 cols = slice(t * P, (t + 1) * P)
@@ -296,56 +296,71 @@ def tile_cauchytransferfunctionfilter_w4_kernel(
                         stop=(g == G - 1),
                     )
 
-        piece_of = {n: (k, piece.index(n)) for k, piece in enumerate(PIECES) for n in piece}
-
-        def make_f(n):
-            k, place = piece_of[n]
+        def make_f(n, parts=slice(0, 2)):
+            count = parts.stop - parts.start
             nc.vector.tensor_tensor(
-                out=f_bf[k,][:, :, P * place : P * (place + 1), :],
-                in0=u_ps[n][:].rearrange("p (o t) d -> p o d t", o=1).to_broadcast([P, 2, P, T]),
-                in1=k_sb[CHUNKS[n][1],][:],
+                out=f_bf[n,][:, parts, :, :],
+                in0=u_ps[n][:].rearrange("p (o t) d -> p o d t", o=1).to_broadcast([P, count, P, T]),
+                in1=k_sb[CHUNKS[n][1],][:, parts, :, :],
                 op=ALU.mult,
             )
 
-        def quant_f(k):
+        def quant_f(n, parts=slice(0, 2)):
             nc.vector.quantize_mx(
-                out=f_codes[k,][:].rearrange("p k d -> p (k d)").bitcast(E4M3),
-                scales=f_sc[k,][:].rearrange("p k d -> p (k d)"),
-                in_=f_bf[k,][:].rearrange("p k d t -> p (k d t)"),
+                out=f_codes[n,][:, parts, :].rearrange("p k d -> p (k d)").bitcast(E4M3),
+                scales=f_sc[n,][:, parts, :].rearrange("p k d -> p (k d)"),
+                in_=f_bf[n,][:, parts, :, :].rearrange("p k d t -> p (k d t)"),
             )
 
-        def synth(k, jj, count, tag="a"):
-            bank = psum.tile([P, count, P * len(PIECES[k])], F32, tag=tag, name="o_ps")
-            o_ps[k, jj] = bank
-            for r in range(count):
-                cols = slice((count * jj + r) * P, (count * jj + r + 1) * P)
-                for c in range(C):
-                    nc.tensor.matmul_mx(
-                        out=bank[:, r, :],
-                        lhsT=q_codes[:, c, cols].bitcast(E4M3),
-                        lhsT_scale=q_sc[:, c, cols],
-                        rhs=f_codes[k,][:, c, :].bitcast(E4M3),
-                        rhs_scale=f_sc[k,][:, c, :],
-                        start=(c == 0),
-                        stop=(c == C - 1),
-                    )
+        def open_bank(k, first, count, tag):
+            bank = psum.tile([P, count, P], F32, tag=tag, name="o_ps")
+            o_ps[k, first] = bank
 
-        def store(k, jj, engine="scalar"):
-            i, ch = CHUNKS[PIECES[k][0]]
-            bank = o_ps[k, jj]
-            count, width = bank.shape[1], bank.shape[2]
-            o_sb = outp.tile([P, count, width], F32)
+        def synth_pass(k, first, r, c, start, stop):
+            cols = slice((first + r) * P, (first + r + 1) * P)
+            nc.tensor.matmul_mx(
+                out=o_ps[k, first][:, r, :],
+                lhsT=q_codes[:, c, cols].bitcast(E4M3),
+                lhsT_scale=q_sc[:, c, cols],
+                rhs=f_codes[k,][:, c, :].bitcast(E4M3),
+                rhs_scale=f_sc[k,][:, c, :],
+                start=start,
+                stop=stop,
+            )
+
+        def store(k, first, engine="scalar"):
+            i, ch = CHUNKS[k]
+            bank = o_ps[k, first]
+            count = bank.shape[1]
+            o_sb = outp.tile([P, count, P], F32)
             drain(o_sb[:], bank[:], engine)
-            rows = out[i].rearrange("(p j) d -> p j d", j=J)[:, count * jj : count * (jj + 1), ch * P : ch * P + width]
+            rows = out[i].rearrange("(p j) d -> p j d", j=J)[:, first : first + count, ch * P : (ch + 1) * P]
             nc.sync.dma_start(out=rows, in_=o_sb[:])
 
+        def banks_of(k):
+            if k == len(CHUNKS) - 1:
+                return [(0, 2, "u"), (2, 2, "u"), (4, 2, "a"), (6, 2, "a")]
+            if k >= 5:
+                return [(0, 2, "u"), (2, 3, "a"), (5, 3, "a")]
+            return [(0, 4, "a"), (4, 4, "a")]
+
         def synth_chunk(k):
-            for jj in range(2):
-                synth(k, jj, 4)
+            for first, count, tag in banks_of(k):
+                open_bank(k, first, count, tag)
+                for r in range(count):
+                    for c in range(C):
+                        synth_pass(k, first, r, c, c == 0, c == C - 1)
+
+        def synth_part(k, c):
+            for first, count, tag in banks_of(k):
+                if c == 0:
+                    open_bank(k, first, count, tag)
+                for r in range(count):
+                    synth_pass(k, first, r, c, c == 0 and r == 0, c == C - 1 and r == count - 1)
 
         def store_chunk(k):
-            for jj in range(2):
-                store(k, jj)
+            for first, count, tag in banks_of(k):
+                store(k, first)
 
         def make_transfer(ch):
             for part in "ir":
@@ -450,14 +465,15 @@ def tile_cauchytransferfunctionfilter_w4_kernel(
         synth_chunk(0)
         store_chunk(0)
         make_f(1)
+        make_transfer(3)
         widen_x(UNITS[2], 1, "vector")
         for n in range(2, last):
             if n > 2:
                 store_chunk(n - 2)
             if n in (2, 3):
                 widen_x(UNITS[3], n - 2, "scalar")
-            if n == 3:
-                transfer(3)
+            if n == 4:
+                drain_transfer(3)
             quant_f(n - 1)
             synth_chunk(n - 1)
             if n + 2 <= last:
@@ -473,6 +489,6 @@ def tile_cauchytransferfunctionfilter_w4_kernel(
         store_chunk(last - 1)
         make_f(last)
         quant_f(last)
-        for jj in range(4):
-            synth(last, jj, 2, "uuaa"[jj])
-            store(last, jj, "vector" if jj % 2 else "scalar")
+        synth_chunk(last)
+        for place, (first, count, tag) in enumerate(banks_of(last)):
+            store(last, first, "vector" if place % 2 else "scalar")

@@ -24,8 +24,19 @@ G = S // (P * T)
 J = S // P
 H = 256
 UNITS = [(0, 0), (1, 0), (0, 1), (1, 1)]
-CHUNKS = [(i, 2 * h + k) for i, h in UNITS for k in range(2)]
-PIECES = [[n] for n in range(len(CHUNKS))]
+CHUNKS = [(0, 0), (1, 0), (0, 1), (1, 1), (0, 2), (0, 3), (1, 2), (1, 3)]
+PIECES = [[0, 1], [2], [3], [4], [5], [6], [7]]
+U_BANKS = [0, 2, 1, 3, 3, 1, 3, 1]
+K_BANKS = [(3, 0), (1, 2), (0, 0), (0, 2)]
+OUT_BANKS = [
+    [(0, 2, 4), (2, 2, 5), (4, 2, 6), (6, 2, 7)],
+    [(0, 4, 4), (4, 4, 5)],
+    [(0, 4, 6), (4, 4, 7)],
+    [(0, 4, 4), (4, 4, 5)],
+    [(0, 2, 0), (2, 3, 6), (5, 3, 7)],
+    [(0, 2, 2), (2, 3, 4), (5, 3, 5)],
+    [(0, 2, 3), (2, 2, 1), (4, 2, 6), (6, 2, 7)],
+]
 
 
 def tile_cauchytransferfunctionfilter_w4_kernel(
@@ -36,7 +47,7 @@ def tile_cauchytransferfunctionfilter_w4_kernel(
         keep = ctx.enter_context(tc.tile_pool(name="keep", bufs=1))
         stage = ctx.enter_context(tc.tile_pool(name="stage", bufs=1))
         outp = ctx.enter_context(tc.tile_pool(name="outp", bufs=8))
-        psum = ctx.enter_context(tc.psum_pool(name="psum", bufs=4))
+        psum = ctx.enter_context(tc.psum_pool(name="psum", bufs=1))
         ctx.enter_context(tc.manual_schedule())
 
         def tiles(name, keys, shape, dtype):
@@ -61,7 +72,11 @@ def tile_cauchytransferfunctionfilter_w4_kernel(
         c_scale = keep.tile([P, D], U8, align_bytes=64)
         x_raw = tiles("x_raw", [(i, g) for i in range(B) for g in range(G)], [P, T * D], U8)
         q_raw = tiles("q_raw", [(c, hs) for c in range(C) for hs in range(2)], [P, J // 2, M], BF16)
-        q_bf = tiles("q_bf", [(c, hs) for c in range(C) for hs in range(2)], [P, S // 2, T], BF16)
+        q_bf = {}
+        for c in range(C):
+            for hs in range(2):
+                q_words = stage.tile([P, S // 2, T], BF16, tag="q_%d_%d" % (c, hs), name="q_bf", align_bytes=64)
+                q_bf[c, hs] = q_words
         q_codes = keep.tile([P, C, S], U32, align_bytes=64)
         q_sc = keep.tile([P, C, S], U8, align_bytes=64)
         root = keep.tile([P, T, M], F32)
@@ -70,7 +85,8 @@ def tile_cauchytransferfunctionfilter_w4_kernel(
         g_bf = tiles("g_bf", parts, [P, M, T], BF16)
         g_codes = tiles("g_codes", parts, [P, M], U32)
         g_sc = tiles("g_sc", parts, [P, M], U8)
-        k_sb = tiles("k_sb", [(ch,) for ch in range(D // P)], [P, 2, P, T], F32)
+        u_sb = tiles("u_sb", CHUNKS[:4], [P, P, T], F32)
+        k_sb = tiles("k_sb", [(2,), (3,)], [P, 2, P, T], F32)
         wide = tiles("wide", UNITS, [P, G, T, H], BF16)
         inter = {}
         x_codes = tiles("x_codes", CHUNKS, [P, G, P], U32)
@@ -107,7 +123,7 @@ def tile_cauchytransferfunctionfilter_w4_kernel(
                 )
 
         def make_de(tm):
-            bank = psum.tile([P, T, P], F32, tag="u", name="de_ps")
+            bank = psum.tile([P, T, P], F32, tag="b%d" % tm, name="de_ps")
             de_ps[tm] = bank
             for t in range(T):
                 nc.tensor.matmul(
@@ -193,27 +209,27 @@ def tile_cauchytransferfunctionfilter_w4_kernel(
             i, ch = CHUNKS[n]
             return wide[i, ch // 2][:, :, :, P * (ch % 2) : P * (ch % 2 + 1)]
 
-        def interleave_x(n):
-            dst = keep.tile([P, G, P, T], BF16, name="inter_%d" % n, align_bytes=64)
-            inter[n] = [(slice(0, G), dst[:].rearrange("p g d t -> p (g d t)"))]
-            nc.vector.tensor_copy(
-                out=dst[:].rearrange("p g (c e) t -> p g c t e", e=4),
-                in_=chunk_planes(n).rearrange("p g t (c e) -> p g c t e", e=4),
-            )
-
-        def interleave_pass(n, g, engine):
-            src = chunk_planes(n)[:, g, :, :]
-            if g == 0:
-                dst = keep.tile([P, P, T], BF16, name="inter_%d" % n, align_bytes=64)
-            else:
-                dst = stage.tile([P, P, T], BF16, tag="f_%d" % (n - 3), name="inter", align_bytes=64)
-            inter.setdefault(n, []).append((slice(g, g + 1), dst[:].rearrange("p d t -> p (d t)")))
+        def interleave_x(n, passes, engine, spent=None):
+            count = passes.stop - passes.start
+            src = chunk_planes(n)[:, passes, :, :]
+            if spent is None:
+                spent = "x_%d_%d" % (n, passes.start)
+            dst = stage.tile([P, count, P, T], BF16, tag=spent, name="inter", align_bytes=64)
+            inter.setdefault(n, []).append((passes, dst[:].rearrange("p g d t -> p (g d t)")))
             if engine == "gpsimd":
                 nc.gpsimd.tensor_scalar(
-                    out=dst[:], in0=src.rearrange("p t d -> p d t"), scalar1=1.0, scalar2=0.0, op0=ALU.mult, op1=ALU.add
+                    out=dst[:],
+                    in0=src.rearrange("p g t d -> p g d t"),
+                    scalar1=1.0,
+                    scalar2=0.0,
+                    op0=ALU.mult,
+                    op1=ALU.add,
                 )
             else:
-                nc.vector.tensor_copy(out=out_runs(dst[:]), in_=in_runs(src))
+                nc.vector.tensor_copy(
+                    out=dst[:].rearrange("p g (c e) t -> p g c t e", e=4),
+                    in_=src.rearrange("p g t (c e) -> p g c t e", e=4),
+                )
 
         def quant_x(n):
             chunk = CHUNKS[n]
@@ -231,7 +247,7 @@ def tile_cauchytransferfunctionfilter_w4_kernel(
                 nc.scalar.copy(out=out_view, in_=in_view)
 
         def turn_q(c, hs, jj):
-            bank = psum.tile([P, 2, 2, P], F32, tag="a", name="q_ps")
+            bank = psum.tile([P, 2, 2, P], F32, tag="b%d" % (4 + 2 * c + jj), name="q_ps")
             q_ps[c, hs, jj] = bank
             words = q_raw[c, hs][:].rearrange("p j m -> p (j m)").bitcast(F32)
             for k in range(2):
@@ -257,32 +273,25 @@ def tile_cauchytransferfunctionfilter_w4_kernel(
                 in_=q_bf[c, hs][:].rearrange("p s t -> p (s t)"),
             )
 
-        def make_k(part, ch):
-            bank = psum.tile([P, T, P], F32, tag="u" if ch == D // P - 1 else "a", name="k_ps")
-            k_ps[part, ch] = bank
-            for t in range(T):
-                cols = slice(t * P, (t + 1) * P)
-                nc.tensor.matmul_mx(
-                    out=bank[:, t, :],
-                    lhsT=g_codes[part,][:, cols].bitcast(E4M3),
-                    lhsT_scale=g_sc[part,][:, cols],
-                    rhs=c_raw[:, 2 * P * ch : 2 * P * (ch + 1)].bitcast(E2M1),
-                    rhs_scale=c_scale[:, P * ch : P * (ch + 1)],
-                    start=True,
-                    stop=True,
-                )
-
-        def drain_k(part, ch):
-            nc.scalar.copy(out=k_sb[ch,][:, "ri".index(part), :, :], in_=k_ps[part, ch][:].rearrange("p t d -> p d t"))
-
-        def transfer(ch):
-            for part in "ir":
-                make_k(part, ch)
-                drain_k(part, ch)
+        def make_k(ch, parts="ir"):
+            for part in parts:
+                bank = psum.tile([P, T, P], F32, tag="b%d" % K_BANKS[ch]["ir".index(part)], name="k_ps")
+                k_ps[part, ch] = bank
+                for t in range(T):
+                    cols = slice(t * P, (t + 1) * P)
+                    nc.tensor.matmul_mx(
+                        out=bank[:, t, :],
+                        lhsT=g_codes[part,][:, cols].bitcast(E4M3),
+                        lhsT_scale=g_sc[part,][:, cols],
+                        rhs=c_raw[:, 2 * P * ch : 2 * P * (ch + 1)].bitcast(E2M1),
+                        rhs_scale=c_scale[:, P * ch : P * (ch + 1)],
+                        start=True,
+                        stop=True,
+                    )
 
         def make_u(n):
             chunk = CHUNKS[n]
-            bank = psum.tile([P, T, P], F32, tag="u", name="u_ps")
+            bank = psum.tile([P, T, P], F32, tag="b%d" % U_BANKS[n], name="u_ps")
             u_ps[n] = bank
             for t in range(T):
                 for g in range(G):
@@ -296,79 +305,86 @@ def tile_cauchytransferfunctionfilter_w4_kernel(
                         stop=(g == G - 1),
                     )
 
-        def make_f(n, parts=slice(0, 2)):
-            count = parts.stop - parts.start
-            nc.vector.tensor_tensor(
-                out=f_bf[n,][:, parts, :, :],
-                in0=u_ps[n][:].rearrange("p (o t) d -> p o d t", o=1).to_broadcast([P, count, P, T]),
-                in1=k_sb[CHUNKS[n][1],][:, parts, :, :],
-                op=ALU.mult,
-            )
+        def drain_u(n):
+            nc.scalar.copy(out=u_sb[CHUNKS[n]][:], in_=u_ps[n][:].rearrange("p t d -> p d t"))
 
-        def quant_f(n, parts=slice(0, 2)):
+        piece_of = {n: (k, piece.index(n)) for k, piece in enumerate(PIECES) for n in piece}
+
+        def drain_k(ch, parts="ir"):
+            for part in parts:
+                nc.scalar.copy(
+                    out=k_sb[ch,][:, "ri".index(part), :, :], in_=k_ps[part, ch][:].rearrange("p t d -> p d t")
+                )
+
+        def make_f(n):
+            k, place = piece_of[n]
+            if CHUNKS[n] not in u_sb:
+                nc.vector.tensor_tensor(
+                    out=f_bf[k,][:],
+                    in0=u_ps[n][:].rearrange("p (o t) d -> p o d t", o=1).to_broadcast([P, 2, P, T]),
+                    in1=k_sb[CHUNKS[n][1],][:],
+                    op=ALU.mult,
+                )
+                return
+            for c, part in ((1, "i"), (0, "r")):
+                nc.vector.tensor_tensor(
+                    out=f_bf[k,][:, c, P * place : P * (place + 1), :],
+                    in0=k_ps[part, CHUNKS[n][1]][:].rearrange("p t d -> p d t"),
+                    in1=u_sb[CHUNKS[n]][:],
+                    op=ALU.mult,
+                )
+
+        def quant_f(k):
             nc.vector.quantize_mx(
-                out=f_codes[n,][:, parts, :].rearrange("p k d -> p (k d)").bitcast(E4M3),
-                scales=f_sc[n,][:, parts, :].rearrange("p k d -> p (k d)"),
-                in_=f_bf[n,][:, parts, :, :].rearrange("p k d t -> p (k d t)"),
+                out=f_codes[k,][:].rearrange("p k d -> p (k d)").bitcast(E4M3),
+                scales=f_sc[k,][:].rearrange("p k d -> p (k d)"),
+                in_=f_bf[k,][:].rearrange("p k d t -> p (k d t)"),
             )
 
-        def open_bank(k, first, count, tag):
-            bank = psum.tile([P, count, P], F32, tag=tag, name="o_ps")
-            o_ps[k, first] = bank
+        def banks_of(k):
+            return OUT_BANKS[k]
 
-        def synth_pass(k, first, r, c, start, stop):
-            cols = slice((first + r) * P, (first + r + 1) * P)
-            nc.tensor.matmul_mx(
-                out=o_ps[k, first][:, r, :],
-                lhsT=q_codes[:, c, cols].bitcast(E4M3),
-                lhsT_scale=q_sc[:, c, cols],
-                rhs=f_codes[k,][:, c, :].bitcast(E4M3),
-                rhs_scale=f_sc[k,][:, c, :],
-                start=start,
-                stop=stop,
-            )
+        def synth(k, which=slice(None)):
+            for first, count, tag in banks_of(k)[which]:
+                bank = psum.tile([P, count, P * len(PIECES[k])], F32, tag="b%d" % tag, name="o_ps")
+                o_ps[k, first] = bank
+                for r in range(count):
+                    cols = slice((first + r) * P, (first + r + 1) * P)
+                    for c in range(C):
+                        nc.tensor.matmul_mx(
+                            out=bank[:, r, :],
+                            lhsT=q_codes[:, c, cols].bitcast(E4M3),
+                            lhsT_scale=q_sc[:, c, cols],
+                            rhs=f_codes[k,][:, c, :].bitcast(E4M3),
+                            rhs_scale=f_sc[k,][:, c, :],
+                            start=(c == 0),
+                            stop=(c == C - 1),
+                        )
+
+        def out_rows(n, first, count):
+            i, ch = CHUNKS[n]
+            return out[i].rearrange("(p j) d -> p j d", j=J)[:, first : first + count, ch * P : (ch + 1) * P]
 
         def store(k, first, engine="scalar"):
-            i, ch = CHUNKS[k]
             bank = o_ps[k, first]
             count = bank.shape[1]
             o_sb = outp.tile([P, count, P], F32)
             drain(o_sb[:], bank[:], engine)
-            rows = out[i].rearrange("(p j) d -> p j d", j=J)[:, first : first + count, ch * P : (ch + 1) * P]
-            nc.sync.dma_start(out=rows, in_=o_sb[:])
+            nc.sync.dma_start(out=out_rows(PIECES[k][0], first, count), in_=o_sb[:])
 
-        def banks_of(k):
-            if k == len(CHUNKS) - 1:
-                return [(0, 2, "u"), (2, 2, "u"), (4, 2, "a"), (6, 2, "a")]
-            if k >= 5:
-                return [(0, 2, "u"), (2, 3, "a"), (5, 3, "a")]
-            return [(0, 4, "a"), (4, 4, "a")]
+        def store_pair(k, half):
+            o_two = outp.tile([P, B, 4, P], F32, bufs=3)
+            for r in range(2):
+                bank = o_ps[k, 4 * half + 2 * r]
+                nc.scalar.copy(
+                    out=o_two[:, :, 2 * r : 2 * r + 2, :], in_=bank[:].rearrange("p r (i d) -> p i r d", i=B)
+                )
+            for i in range(B):
+                nc.sync.dma_start(out=out_rows(PIECES[k][i], 4 * half, 4), in_=o_two[:, i, :, :])
 
-        def synth_chunk(k):
-            for first, count, tag in banks_of(k):
-                open_bank(k, first, count, tag)
-                for r in range(count):
-                    for c in range(C):
-                        synth_pass(k, first, r, c, c == 0, c == C - 1)
-
-        def synth_part(k, c):
-            for first, count, tag in banks_of(k):
-                if c == 0:
-                    open_bank(k, first, count, tag)
-                for r in range(count):
-                    synth_pass(k, first, r, c, c == 0 and r == 0, c == C - 1 and r == count - 1)
-
-        def store_chunk(k):
+        def store_piece(k):
             for first, count, tag in banks_of(k):
                 store(k, first)
-
-        def make_transfer(ch):
-            for part in "ir":
-                make_k(part, ch)
-
-        def drain_transfer(ch):
-            for part in "ir":
-                drain_k(part, ch)
 
         nc.sync.dma_start(out=rhs_rows[31:32, :], in_=om.rearrange("(o m) -> o m", o=1))
         nc.sync.dma_start(out=lhs_rows[63:64, :], in_=nu.rearrange("(o n) -> o n", o=1))
@@ -392,14 +408,15 @@ def tile_cauchytransferfunctionfilter_w4_kernel(
         nc.vector.memset(c_scale[:].bitcast(I32), 0)
 
         load_p_scales()
-        load_q(1, 0)
         load_x(1, 0)
         load_x(1, 1)
+        load_q(1, 0)
         load_q(0, 1)
         nc.sync.dma_start(out=c_raw[:], in_=c_words[0])
         load_c_scales()
         load_q(1, 1)
 
+        both, first_pass, second_pass = slice(0, G), slice(0, 1), slice(1, G)
         q_banks = [(c, hs, jj) for hs in range(2) for c in range(C) for jj in range(2)]
         for tm in range(T):
             make_de(tm)
@@ -412,83 +429,96 @@ def tile_cauchytransferfunctionfilter_w4_kernel(
         widen_x(UNITS[2], 0, "scalar", range(1))
         make_root(1)
         for g in range(G):
+            widen_x(UNITS[1], g, "scalar")
+        for g in range(G):
             widen_x(UNITS[0], g, "vector")
         permute_p()
-        interleave_x(0)
-        interleave_x(1)
+        interleave_x(0, both, "vector")
+        interleave_x(2, both, "vector")
         quant_x(0)
         make_w(0)
-        quant_x(1)
+        permute_p_scales()
         make_gr(0, "gpsimd")
         make_gi(0)
         make_gi(1)
-        for bank in q_banks[:4]:
-            drain_q(*bank, "scalar")
         make_gr(1, "scalar")
+        make_u(0)
         make_w(1)
-        permute_p_scales()
+        quant_x(2)
+        make_u(2)
         make_gr(2, "gpsimd")
         make_gi(2)
         make_gi(3)
-        widen_x(UNITS[1], 0, "scalar")
+        for bank in q_banks[:2]:
+            drain_q(*bank, "scalar")
         make_gr(3, "scalar")
-        widen_x(UNITS[1], 1, "scalar")
+        for bank in q_banks[2:4]:
+            drain_q(*bank, "scalar")
         for bank in q_banks[4:6]:
             turn_q(*bank)
-            drain_q(*bank, "scalar")
-        make_u(0)
-        make_u(1)
-        quant_q(0, 0)
+        drain_u(0)
+        drain_u(2)
+        interleave_x(1, both, "vector")
         quant_g("i")
+        quant_x(1)
+        make_u(1)
         quant_g("r")
-        transfer(0)
+        make_k(0)
+        drain_u(1)
+        for bank in q_banks[4:6]:
+            drain_q(*bank, "scalar")
         for bank in q_banks[6:]:
             turn_q(*bank)
             drain_q(*bank, "scalar")
-        transfer(1)
+        make_k(1)
+        quant_q(0, 0)
+        interleave_x(3, both, "gpsimd", "q_0_0")
         quant_q(1, 0)
-        interleave_x(2)
-        interleave_x(3)
-        quant_x(2)
-        make_u(2)
+        make_f(0)
+        make_f(1)
+        make_k(2, "i")
         quant_x(3)
         make_u(3)
-        make_transfer(2)
-        widen_x(UNITS[2], 0, "scalar", range(1, T))
-
-        last = len(CHUNKS) - 1
-        quant_q(0, 1)
-        make_f(0)
-        quant_q(1, 1)
         quant_f(0)
-        drain_transfer(2)
-        synth_chunk(0)
-        store_chunk(0)
-        make_f(1)
-        make_transfer(3)
+        quant_q(0, 1)
+        quant_q(1, 1)
+        widen_x(UNITS[2], 0, "scalar", range(1, T))
+        drain_k(2, "i")
+        drain_u(3)
+        synth(0, slice(0, 2))
+        make_k(2, "r")
+        synth(0, slice(2, 4))
         widen_x(UNITS[2], 1, "vector")
+        store_pair(0, 0)
+        widen_x(UNITS[3], 0, "scalar")
+        drain_k(2, "r")
+        store_pair(0, 1)
+        widen_x(UNITS[3], 1, "scalar", range(3))
+        last = len(CHUNKS) - 1
         for n in range(2, last):
             if n > 2:
-                store_chunk(n - 2)
-            if n in (2, 3):
-                widen_x(UNITS[3], n - 2, "scalar")
+                quant_f(n - 2)
+                synth(n - 2)
             if n == 4:
-                drain_transfer(3)
-            quant_f(n - 1)
-            synth_chunk(n - 1)
+                drain_k(3)
             if n + 2 <= last:
-                interleave_pass(n + 2, 0, "vector")
-                interleave_pass(n + 2, 1, "gpsimd")
+                interleave_x(n + 2, first_pass, "vector")
+                interleave_x(n + 2, second_pass, "gpsimd", "f_%d" % (n - 2) if n > 2 else "q_1_1")
             make_f(n)
+            if n == 3:
+                make_k(3)
             if n + 2 <= last:
                 quant_x(n + 2)
                 make_u(n + 2)
-        store_chunk(last - 2)
-        quant_f(last - 1)
-        synth_chunk(last - 1)
-        store_chunk(last - 1)
+            if n == 2:
+                widen_x(UNITS[3], 1, "vector", range(3, T))
+            if n > 2:
+                store_piece(n - 2)
+        quant_f(last - 2)
+        synth(last - 2)
+        store_piece(last - 2)
         make_f(last)
-        quant_f(last)
-        synth_chunk(last)
-        for place, (first, count, tag) in enumerate(banks_of(last)):
-            store(last, first, "vector" if place % 2 else "scalar")
+        quant_f(last - 1)
+        synth(last - 1)
+        for place, (first, count, tag) in enumerate(banks_of(last - 1)):
+            store(last - 1, first, "vector" if place % 2 else "scalar")

@@ -33,8 +33,8 @@ OUT_BANKS = [
     [(0, 4, 4), (4, 4, 5)],
     [(0, 4, 6), (4, 4, 7)],
     [(0, 4, 4), (4, 4, 5)],
-    [(0, 2, 0), (2, 3, 6), (5, 3, 7)],
-    [(0, 2, 2), (2, 3, 4), (5, 3, 5)],
+    [(0, 2, 0), (2, 2, 2), (4, 2, 6), (6, 2, 7)],
+    [(0, 2, 0), (2, 3, 4), (5, 3, 5)],
     [(0, 2, 3), (2, 2, 1), (4, 2, 6), (6, 2, 7)],
 ]
 
@@ -318,19 +318,16 @@ def tile_cauchytransferfunctionfilter_w4_kernel(
 
         def make_f(n):
             k, place = piece_of[n]
-            if CHUNKS[n] not in u_sb:
-                nc.vector.tensor_tensor(
-                    out=f_bf[k,][:],
-                    in0=u_ps[n][:].rearrange("p (o t) d -> p o d t", o=1).to_broadcast([P, 2, P, T]),
-                    in1=k_sb[CHUNKS[n][1],][:],
-                    op=ALU.mult,
-                )
-                return
+            ch = CHUNKS[n][1]
             for c, part in ((1, "i"), (0, "r")):
+                if CHUNKS[n] in u_sb:
+                    in_psum, in_sbuf = k_ps[part, ch], u_sb[CHUNKS[n]][:]
+                else:
+                    in_psum, in_sbuf = u_ps[n], k_sb[ch,][:, c, :, :]
                 nc.vector.tensor_tensor(
                     out=f_bf[k,][:, c, P * place : P * (place + 1), :],
-                    in0=k_ps[part, CHUNKS[n][1]][:].rearrange("p t d -> p d t"),
-                    in1=u_sb[CHUNKS[n]][:],
+                    in0=in_psum[:].rearrange("p t d -> p d t"),
+                    in1=in_sbuf,
                     op=ALU.mult,
                 )
 

@@ -25,7 +25,10 @@ J = S // P
 H = 256
 UNITS = [(0, 0), (1, 0), (0, 1), (1, 1)]
 CHUNKS = [(0, 0), (1, 0), (0, 1), (1, 1), (0, 2), (0, 3), (1, 2), (1, 3)]
+K_IN_PSUM = 4
 PIECES = [[0, 1], [2], [3], [4], [5], [6], [7]]
+LAST_PASS_ON_SCALAR = 3
+
 U_BANKS = [0, 2, 1, 3, 3, 1, 3, 1]
 K_BANKS = [(3, 0), (1, 2), (0, 0), (0, 2)]
 OUT_BANKS = [
@@ -85,7 +88,7 @@ def tile_cauchytransferfunctionfilter_w4_kernel(
         g_bf = tiles("g_bf", parts, [P, M, T], BF16)
         g_codes = tiles("g_codes", parts, [P, M], U32)
         g_sc = tiles("g_sc", parts, [P, M], U8)
-        u_sb = tiles("u_sb", CHUNKS[:4], [P, P, T], F32)
+        u_sb = tiles("u_sb", CHUNKS[:K_IN_PSUM], [P, P, T], F32)
         k_sb = tiles("k_sb", [(2,), (3,)], [P, 2, P, T], F32)
         wide = tiles("wide", UNITS, [P, G, T, H], BF16)
         inter = {}
@@ -240,12 +243,6 @@ def tile_cauchytransferfunctionfilter_w4_kernel(
                     in_=words,
                 )
 
-        def drain(out_view, in_view, engine):
-            if engine == "vector":
-                nc.vector.tensor_copy(out=out_view, in_=in_view)
-            else:
-                nc.scalar.copy(out=out_view, in_=in_view)
-
         def turn_q(c, hs, jj):
             bank = psum.tile([P, 2, 2, P], F32, tag="b%d" % (4 + 2 * c + jj), name="q_ps")
             q_ps[c, hs, jj] = bank
@@ -255,14 +252,13 @@ def tile_cauchytransferfunctionfilter_w4_kernel(
                 for u in range(2):
                     nc.tensor.transpose(bank[:, k, u, :], words[:, base + u : base + M // 2 : 2], ident[:])
 
-        def drain_q(c, hs, jj, engine):
-            drain(
-                q_bf[c, hs][:, 2 * jj * P : (2 * jj + 2) * P, :]
+        def drain_q(c, hs, jj):
+            nc.scalar.copy(
+                out=q_bf[c, hs][:, 2 * jj * P : (2 * jj + 2) * P, :]
                 .rearrange("p s t -> p (s t)")
                 .bitcast(F32)
                 .rearrange("p (k s u) -> p k s u", k=2, u=2),
-                q_ps[c, hs, jj][:].rearrange("p k u s -> p k s u"),
-                engine,
+                in_=q_ps[c, hs, jj][:].rearrange("p k u s -> p k s u"),
             )
 
         def quant_q(c, hs):
@@ -289,6 +285,12 @@ def tile_cauchytransferfunctionfilter_w4_kernel(
                         stop=True,
                     )
 
+        def drain_k(ch, parts="ir"):
+            for part in parts:
+                nc.scalar.copy(
+                    out=k_sb[ch,][:, "ri".index(part), :, :], in_=k_ps[part, ch][:].rearrange("p t d -> p d t")
+                )
+
         def make_u(n):
             chunk = CHUNKS[n]
             bank = psum.tile([P, T, P], F32, tag="b%d" % U_BANKS[n], name="u_ps")
@@ -310,12 +312,6 @@ def tile_cauchytransferfunctionfilter_w4_kernel(
 
         piece_of = {n: (k, piece.index(n)) for k, piece in enumerate(PIECES) for n in piece}
 
-        def drain_k(ch, parts="ir"):
-            for part in parts:
-                nc.scalar.copy(
-                    out=k_sb[ch,][:, "ri".index(part), :, :], in_=k_ps[part, ch][:].rearrange("p t d -> p d t")
-                )
-
         def make_f(n):
             k, place = piece_of[n]
             ch = CHUNKS[n][1]
@@ -331,19 +327,20 @@ def tile_cauchytransferfunctionfilter_w4_kernel(
                     op=ALU.mult,
                 )
 
-        def quant_f(k):
+        def quant_f(k, parts=slice(0, 2)):
             nc.vector.quantize_mx(
-                out=f_codes[k,][:].rearrange("p k d -> p (k d)").bitcast(E4M3),
-                scales=f_sc[k,][:].rearrange("p k d -> p (k d)"),
-                in_=f_bf[k,][:].rearrange("p k d t -> p (k d t)"),
+                out=f_codes[k,][:, parts, :].rearrange("p k d -> p (k d)").bitcast(E4M3),
+                scales=f_sc[k,][:, parts, :].rearrange("p k d -> p (k d)"),
+                in_=f_bf[k,][:, parts, :, :].rearrange("p k d t -> p (k d t)"),
             )
 
-        def banks_of(k):
-            return OUT_BANKS[k]
+        def quant_f_in_parts(k):
+            quant_f(k, slice(1, 2))
+            quant_f(k, slice(0, 1))
 
         def synth(k, which=slice(None)):
-            for first, count, tag in banks_of(k)[which]:
-                bank = psum.tile([P, count, P * len(PIECES[k])], F32, tag="b%d" % tag, name="o_ps")
+            for first, count, number in OUT_BANKS[k][which]:
+                bank = psum.tile([P, count, P * len(PIECES[k])], F32, tag="b%d" % number, name="o_ps")
                 o_ps[k, first] = bank
                 for r in range(count):
                     cols = slice((first + r) * P, (first + r + 1) * P)
@@ -366,7 +363,10 @@ def tile_cauchytransferfunctionfilter_w4_kernel(
             bank = o_ps[k, first]
             count = bank.shape[1]
             o_sb = outp.tile([P, count, P], F32)
-            drain(o_sb[:], bank[:], engine)
+            if engine == "vector":
+                nc.vector.tensor_copy(out=o_sb[:], in_=bank[:])
+            else:
+                nc.scalar.copy(out=o_sb[:], in_=bank[:])
             nc.sync.dma_start(out=out_rows(PIECES[k][0], first, count), in_=o_sb[:])
 
         def store_pair(k, half):
@@ -380,7 +380,7 @@ def tile_cauchytransferfunctionfilter_w4_kernel(
                 nc.sync.dma_start(out=out_rows(PIECES[k][i], 4 * half, 4), in_=o_two[:, i, :, :])
 
         def store_piece(k):
-            for first, count, tag in banks_of(k):
+            for first, _, _ in OUT_BANKS[k]:
                 store(k, first)
 
         nc.sync.dma_start(out=rhs_rows[31:32, :], in_=om.rearrange("(o m) -> o m", o=1))
@@ -447,14 +447,15 @@ def tile_cauchytransferfunctionfilter_w4_kernel(
         make_gi(2)
         make_gi(3)
         for bank in q_banks[:2]:
-            drain_q(*bank, "scalar")
+            drain_q(*bank)
         make_gr(3, "scalar")
         for bank in q_banks[2:4]:
-            drain_q(*bank, "scalar")
+            drain_q(*bank)
         for bank in q_banks[4:6]:
             turn_q(*bank)
         drain_u(0)
         drain_u(2)
+
         interleave_x(1, both, "vector")
         quant_g("i")
         quant_x(1)
@@ -463,10 +464,10 @@ def tile_cauchytransferfunctionfilter_w4_kernel(
         make_k(0)
         drain_u(1)
         for bank in q_banks[4:6]:
-            drain_q(*bank, "scalar")
+            drain_q(*bank)
         for bank in q_banks[6:]:
             turn_q(*bank)
-            drain_q(*bank, "scalar")
+            drain_q(*bank)
         make_k(1)
         quant_q(0, 0)
         interleave_x(3, both, "gpsimd", "q_0_0")
@@ -490,7 +491,8 @@ def tile_cauchytransferfunctionfilter_w4_kernel(
         widen_x(UNITS[3], 0, "scalar")
         drain_k(2, "r")
         store_pair(0, 1)
-        widen_x(UNITS[3], 1, "scalar", range(3))
+        widen_x(UNITS[3], 1, "scalar", range(LAST_PASS_ON_SCALAR))
+
         last = len(CHUNKS) - 1
         for n in range(2, last):
             if n > 2:
@@ -508,14 +510,14 @@ def tile_cauchytransferfunctionfilter_w4_kernel(
                 quant_x(n + 2)
                 make_u(n + 2)
             if n == 2:
-                widen_x(UNITS[3], 1, "vector", range(3, T))
+                widen_x(UNITS[3], 1, "vector", range(LAST_PASS_ON_SCALAR, T))
             if n > 2:
                 store_piece(n - 2)
-        quant_f(last - 2)
+        quant_f_in_parts(last - 2)
         synth(last - 2)
         store_piece(last - 2)
         make_f(last)
-        quant_f(last - 1)
+        quant_f_in_parts(last - 1)
         synth(last - 1)
-        for place, (first, count, tag) in enumerate(banks_of(last - 1)):
+        for place, (first, _, _) in enumerate(OUT_BANKS[last - 1]):
             store(last - 1, first, "vector" if place % 2 else "scalar")

@@ -18,6 +18,9 @@ E2M1 = mybir.dt.float4_e2m1fn_x4
 ALU = mybir.AluOpType
 ACT = mybir.ActivationFunctionType
 
+ONE_TWICE = 0x3F803F80
+MINUS_ONE_TWICE = 0xBF80BF80
+
 P = 128
 T = 4
 G = S // (P * T)
@@ -103,9 +106,10 @@ def tile_cauchytransferfunctionfilter_w4_kernel(
             f_sc.update(tiles("f_sc", [(k,)], [P, 2, width], U8))
         de_ps, q_ps, k_ps, u_ps, o_ps = {}, {}, {}, {}, {}
 
-        def load_x(i, g):
+        def load_x(i, g, slots=slice(0, T)):
             rows = x_bytes[i, g * P * T : (g + 1) * P * T, :].rearrange("(p t) d -> p (t d)", t=T)
-            nc.sync.dma_start(out=x_raw[i, g][:], in_=rows)
+            cols = slice(slots.start * D, slots.stop * D)
+            nc.sync.dma_start(out=x_raw[i, g][:, cols], in_=rows[:, cols])
 
         def load_q(c, hs):
             rows = q[c].rearrange("(p j) m -> p j m", j=J)[:, 4 * hs : 4 * hs + 4, :]
@@ -136,8 +140,8 @@ def tile_cauchytransferfunctionfilter_w4_kernel(
         def square(tm):
             nc.scalar.activation(out=root[:, :, P * tm : P * (tm + 1)], in_=de_ps[tm][:], func=ACT.Square)
 
-        def make_root(hm):
-            cols = slice(256 * hm, 256 * (hm + 1))
+        def make_root(tm):
+            cols = slice(P * tm, P * (tm + 1))
             nc.scalar.activation(
                 out=root[:, :, cols], in_=root[:, :, cols], func=ACT.Abs_reciprocal_sqrt, bias=quarter[:], scale=1.0
             )
@@ -185,10 +189,10 @@ def tile_cauchytransferfunctionfilter_w4_kernel(
                 in_=g_bf[part,][:].rearrange("p m t -> p (m t)"),
             )
 
-        def permute_p():
+        def permute_p(g):
             nc.vector.tensor_copy(
-                out=p_perm[:].bitcast(U16).rearrange("p g (t m) -> p g t m", t=T),
-                in_=p_raw[:].bitcast(U16).rearrange("p g (m t) -> p g t m", t=T),
+                out=p_perm[:, g, :].bitcast(U16).rearrange("p (t m) -> p t m", t=T),
+                in_=p_raw[:, g, :].bitcast(U16).rearrange("p (m t) -> p t m", t=T),
             )
 
         def permute_p_scales():
@@ -383,31 +387,31 @@ def tile_cauchytransferfunctionfilter_w4_kernel(
             for first, _, _ in OUT_BANKS[k]:
                 store(k, first)
 
-        nc.sync.dma_start(out=rhs_rows[31:32, :], in_=om.rearrange("(o m) -> o m", o=1))
-        nc.sync.dma_start(out=lhs_rows[63:64, :], in_=nu.rearrange("(o n) -> o n", o=1))
+        nc.sync.dma_start(out=rhs_rows[63:64, :], in_=om.rearrange("(o m) -> o m", o=1))
+        nc.sync.dma_start(out=lhs_rows[127:128, :], in_=nu.rearrange("(o n) -> o n", o=1))
         nc.sync.dma_start(out=xs[:], in_=x_scale.rearrange("o (g p t) w -> p (o g) (t w)", p=P, t=T))
-        load_x(0, 0)
-        load_x(0, 1)
-        nc.sync.dma_start(out=p_raw[:], in_=p_words.rearrange("g p w -> p g w"))
+        for g in range(G):
+            load_x(0, g, slice(0, 2))
+            load_x(0, g, slice(2, T))
+        for g in range(G):
+            nc.sync.dma_start(out=p_raw[:, g, :], in_=p_words[g])
         nc.sync.dma_start(out=b_col[:], in_=b.rearrange("(p t) -> p t", t=T))
         load_q(0, 0)
 
         make_identity(nc, ident[:])
         nc.vector.memset(quarter[:], 0.25)
         nc.scalar.activation(out=warm[:], in_=quarter[:], func=ACT.Abs_reciprocal_sqrt, bias=quarter[:], scale=1.0)
-        nc.vector.memset(lhs_rows[0:32, :], 1.0)
-        nc.vector.memset(rhs_rows[32:64, :], -1.0)
-        nc.vector.memset(rhs_rows[0:31, :].bitcast(F32), 0.0)
-        nc.vector.memset(lhs_rows[32:63, :].bitcast(F32), 0.0)
-        nc.vector.memset(rhs_rows[64:128, :].bitcast(F32), 0.0)
-        nc.vector.memset(lhs_rows[64:128, :].bitcast(F32), 0.0)
+        nc.vector.memset(lhs_rows[0:64, :].bitcast(U32), ONE_TWICE)
+        nc.vector.memset(rhs_rows[64:128, :].bitcast(U32), MINUS_ONE_TWICE)
+        nc.vector.memset(rhs_rows[0:63, :].bitcast(F32), 0.0)
+        nc.vector.memset(lhs_rows[64:127, :].bitcast(F32), 0.0)
         nc.vector.memset(p_scale_raw[:].rearrange("p g m -> p (g m)").bitcast(I32), 0)
         nc.vector.memset(c_scale[:].bitcast(I32), 0)
 
         load_p_scales()
+        load_q(1, 0)
         load_x(1, 0)
         load_x(1, 1)
-        load_q(1, 0)
         load_q(0, 1)
         nc.sync.dma_start(out=c_raw[:], in_=c_words[0])
         load_c_scales()
@@ -419,17 +423,19 @@ def tile_cauchytransferfunctionfilter_w4_kernel(
             make_de(tm)
         for bank in q_banks[:4]:
             turn_q(*bank)
-        for tm in range(3):
-            square(tm)
-        make_root(0)
-        square(3)
         widen_x(UNITS[2], 0, "scalar", range(1))
-        make_root(1)
+        for pair in ((0, 1), (2, 3)):
+            for tm in pair:
+                square(tm)
+            for tm in pair:
+                make_root(tm)
+        widen_x(UNITS[2], 0, "scalar", range(1, 2))
         for g in range(G):
             widen_x(UNITS[1], g, "scalar")
         for g in range(G):
             widen_x(UNITS[0], g, "vector")
-        permute_p()
+        for g in range(G):
+            permute_p(g)
         interleave_x(0, both, "vector")
         interleave_x(2, both, "vector")
         quant_x(0)
@@ -458,10 +464,11 @@ def tile_cauchytransferfunctionfilter_w4_kernel(
 
         interleave_x(1, both, "vector")
         quant_g("i")
+        make_k(0, "i")
         quant_x(1)
         make_u(1)
         quant_g("r")
-        make_k(0)
+        make_k(0, "r")
         drain_u(1)
         for bank in q_banks[4:6]:
             drain_q(*bank)
@@ -480,7 +487,7 @@ def tile_cauchytransferfunctionfilter_w4_kernel(
         quant_f(0)
         quant_q(0, 1)
         quant_q(1, 1)
-        widen_x(UNITS[2], 0, "scalar", range(1, T))
+        widen_x(UNITS[2], 0, "scalar", range(2, T))
         drain_k(2, "i")
         drain_u(3)
         synth(0, slice(0, 2))
@@ -488,8 +495,9 @@ def tile_cauchytransferfunctionfilter_w4_kernel(
         synth(0, slice(2, 4))
         widen_x(UNITS[2], 1, "vector")
         store_pair(0, 0)
-        widen_x(UNITS[3], 0, "scalar")
         drain_k(2, "r")
+        make_k(3, "i")
+        widen_x(UNITS[3], 0, "scalar")
         store_pair(0, 1)
         widen_x(UNITS[3], 1, "scalar", range(LAST_PASS_ON_SCALAR))
 
@@ -505,7 +513,7 @@ def tile_cauchytransferfunctionfilter_w4_kernel(
                 interleave_x(n + 2, second_pass, "gpsimd", "f_%d" % (n - 2) if n > 2 else "q_1_1")
             make_f(n)
             if n == 3:
-                make_k(3)
+                make_k(3, "r")
             if n + 2 <= last:
                 quant_x(n + 2)
                 make_u(n + 2)

@@ -27,22 +27,9 @@ G = S // (P * T)
 J = S // P
 H = 256
 UNITS = [(0, 0), (1, 0), (0, 1), (1, 1)]
-CHUNKS = [(0, 0), (1, 0), (0, 1), (1, 1), (0, 2), (0, 3), (1, 2), (1, 3)]
-K_IN_PSUM = 4
+CHUNKS = [(i, 2 * h + e) for i, h in UNITS for e in range(2)]
+U_COPIED = [0, 1, 2, 3]
 PIECES = [[0, 1], [2], [3], [4], [5], [6], [7]]
-LAST_PASS_ON_SCALAR = 3
-
-U_BANKS = [0, 2, 1, 3, 3, 1, 3, 1]
-K_BANKS = [(3, 0), (1, 2), (0, 0), (0, 2)]
-OUT_BANKS = [
-    [(0, 2, 4), (2, 2, 5), (4, 2, 6), (6, 2, 7)],
-    [(0, 4, 4), (4, 4, 5)],
-    [(0, 4, 6), (4, 4, 7)],
-    [(0, 4, 4), (4, 4, 5)],
-    [(0, 2, 0), (2, 2, 2), (4, 2, 6), (6, 2, 7)],
-    [(0, 2, 0), (2, 3, 4), (5, 3, 5)],
-    [(0, 2, 3), (2, 2, 1), (4, 2, 6), (6, 2, 7)],
-]
 
 
 def tile_cauchytransferfunctionfilter_w4_kernel(
@@ -52,7 +39,7 @@ def tile_cauchytransferfunctionfilter_w4_kernel(
     with ExitStack() as ctx:
         keep = ctx.enter_context(tc.tile_pool(name="keep", bufs=1))
         stage = ctx.enter_context(tc.tile_pool(name="stage", bufs=1))
-        outp = ctx.enter_context(tc.tile_pool(name="outp", bufs=8))
+        outp = ctx.enter_context(tc.tile_pool(name="outp", bufs=12))
         psum = ctx.enter_context(tc.psum_pool(name="psum", bufs=1))
         ctx.enter_context(tc.manual_schedule())
 
@@ -88,10 +75,13 @@ def tile_cauchytransferfunctionfilter_w4_kernel(
         root = keep.tile([P, T, M], F32)
         w = keep.tile([P, T, M], F32)
         parts = [("r",), ("i",)]
-        g_bf = tiles("g_bf", parts, [P, M, T], BF16)
+        g_bf = {}
+        for key in parts:
+            g_words = stage.tile([P, M, T], BF16, tag="g_" + key[0], name="g_bf", align_bytes=64)
+            g_bf[key] = g_words
         g_codes = tiles("g_codes", parts, [P, M], U32)
         g_sc = tiles("g_sc", parts, [P, M], U8)
-        u_sb = tiles("u_sb", CHUNKS[:K_IN_PSUM], [P, P, T], F32)
+        u_sb = tiles("u_sb", [CHUNKS[n] for n in U_COPIED], [P, P, T], F32)
         k_sb = tiles("k_sb", [(2,), (3,)], [P, 2, P, T], F32)
         wide = tiles("wide", UNITS, [P, G, T, H], BF16)
         inter = {}
@@ -164,8 +154,8 @@ def tile_cauchytransferfunctionfilter_w4_kernel(
         def out_runs(words):
             return words.rearrange("p (c e) t -> p c t e", e=4)
 
-        def make_gr(tm, engine):
-            cols = slice(P * tm, P * (tm + 1))
+        def make_gr(first, count, engine):
+            cols = slice(P * first, P * (first + count))
             dst, src = g_bf["r",][:, cols, :], w[:, :, cols]
             if engine == "scalar":
                 nc.scalar.activation(out=out_runs(dst), in_=in_runs(src), func=ACT.Copy, scale=0.5)
@@ -201,28 +191,29 @@ def tile_cauchytransferfunctionfilter_w4_kernel(
                 in_=p_scale_raw[:].rearrange("p g (m t) -> p g t m", t=T),
             )
 
-        def widen_x(unit, g, engine, slots=range(T)):
-            i, h = unit
+        def widen_x(unit, g, engine, slots=range(T), cols=slice(0, H)):
+            i, h = UNITS[unit]
             for t in slots:
-                src = x_raw[i, g][:, t * D + h * H : t * D + (h + 1) * H].bitcast(F8)
+                src = x_raw[i, g][:, t * D + h * H + cols.start : t * D + h * H + cols.stop].bitcast(F8)
                 scale = xs[:, g, t : t + 1]
-                dst = wide[unit][:, g, t, :]
+                dst = wide[i, h][:, g, t, cols]
                 if engine == "vector":
                     nc.vector.tensor_scalar(out=dst, in0=src, scalar1=scale, scalar2=None, op0=ALU.mult)
                 else:
                     nc.scalar.activation(out=dst, in_=src, func=ACT.Copy, scale=scale)
 
-        def chunk_planes(n):
-            i, ch = CHUNKS[n]
-            return wide[i, ch // 2][:, :, :, P * (ch % 2) : P * (ch % 2 + 1)]
-
-        def interleave_x(n, passes, engine, spent=None):
-            count = passes.stop - passes.start
-            src = chunk_planes(n)[:, passes, :, :]
+        def interleave_x(unit, passes, cols, engine, spent=None):
+            src = wide[UNITS[unit]][:, passes, :, cols]
             if spent is None:
-                spent = "x_%d_%d" % (n, passes.start)
-            dst = stage.tile([P, count, P, T], BF16, tag=spent, name="inter", align_bytes=64)
-            inter.setdefault(n, []).append((passes, dst[:].rearrange("p g d t -> p (g d t)")))
+                spent = "x_%d_%d_%d" % (unit, passes.start, cols.start)
+            shape = [P, passes.stop - passes.start, cols.stop - cols.start, T]
+            dst = stage.tile(shape, BF16, tag=spent, name="inter", align_bytes=64)
+            for e in range(2):
+                lo, hi = max(cols.start, P * e), min(cols.stop, P * (e + 1))
+                if lo < hi:
+                    part = dst[:, :, lo - cols.start : hi - cols.start, :]
+                    whole = hi - lo == P and shape[2] == P
+                    inter.setdefault(2 * unit + e, []).append((passes, slice(lo - P * e, hi - P * e), part, whole))
             if engine == "gpsimd":
                 nc.gpsimd.tensor_scalar(
                     out=dst[:],
@@ -240,15 +231,23 @@ def tile_cauchytransferfunctionfilter_w4_kernel(
 
         def quant_x(n):
             chunk = CHUNKS[n]
-            for passes, words in inter[n]:
-                nc.vector.quantize_mx(
-                    out=x_codes[chunk][:, passes, :].rearrange("p g d -> p (g d)").bitcast(E4M3),
-                    scales=x_sc[chunk][:, passes, :].rearrange("p g d -> p (g d)"),
-                    in_=words,
-                )
+            for passes, cols, words, whole in inter[n]:
+                if whole:
+                    nc.vector.quantize_mx(
+                        out=x_codes[chunk][:, passes, :].rearrange("p g d -> p (g d)").bitcast(E4M3),
+                        scales=x_sc[chunk][:, passes, :].rearrange("p g d -> p (g d)"),
+                        in_=words.rearrange("p g d t -> p (g d t)"),
+                    )
+                else:
+                    for g in range(passes.start, passes.stop):
+                        nc.vector.quantize_mx(
+                            out=x_codes[chunk][:, g, cols].bitcast(E4M3),
+                            scales=x_sc[chunk][:, g, cols],
+                            in_=words[:, g - passes.start, :, :].rearrange("p d t -> p (d t)"),
+                        )
 
-        def turn_q(c, hs, jj):
-            bank = psum.tile([P, 2, 2, P], F32, tag="b%d" % (4 + 2 * c + jj), name="q_ps")
+        def turn_q(c, hs, jj, number):
+            bank = psum.tile([P, 2, 2, P], F32, tag="b%d" % number, name="q_ps")
             q_ps[c, hs, jj] = bank
             words = q_raw[c, hs][:].rearrange("p j m -> p (j m)").bitcast(F32)
             for k in range(2):
@@ -273,9 +272,9 @@ def tile_cauchytransferfunctionfilter_w4_kernel(
                 in_=q_bf[c, hs][:].rearrange("p s t -> p (s t)"),
             )
 
-        def make_k(ch, parts="ir"):
-            for part in parts:
-                bank = psum.tile([P, T, P], F32, tag="b%d" % K_BANKS[ch]["ir".index(part)], name="k_ps")
+        def make_k(ch, part, number):
+            if True:
+                bank = psum.tile([P, T, P], F32, tag="b%d" % number, name="k_ps")
                 k_ps[part, ch] = bank
                 for t in range(T):
                     cols = slice(t * P, (t + 1) * P)
@@ -295,9 +294,9 @@ def tile_cauchytransferfunctionfilter_w4_kernel(
                     out=k_sb[ch,][:, "ri".index(part), :, :], in_=k_ps[part, ch][:].rearrange("p t d -> p d t")
                 )
 
-        def make_u(n):
+        def make_u(n, number):
             chunk = CHUNKS[n]
-            bank = psum.tile([P, T, P], F32, tag="b%d" % U_BANKS[n], name="u_ps")
+            bank = psum.tile([P, T, P], F32, tag="b%d" % number, name="u_ps")
             u_ps[n] = bank
             for t in range(T):
                 for g in range(G):
@@ -342,50 +341,33 @@ def tile_cauchytransferfunctionfilter_w4_kernel(
             quant_f(k, slice(1, 2))
             quant_f(k, slice(0, 1))
 
-        def synth(k, which=slice(None)):
-            for first, count, number in OUT_BANKS[k][which]:
-                bank = psum.tile([P, count, P * len(PIECES[k])], F32, tag="b%d" % number, name="o_ps")
-                o_ps[k, first] = bank
-                for r in range(count):
-                    cols = slice((first + r) * P, (first + r + 1) * P)
-                    for c in range(C):
-                        nc.tensor.matmul_mx(
-                            out=bank[:, r, :],
-                            lhsT=q_codes[:, c, cols].bitcast(E4M3),
-                            lhsT_scale=q_sc[:, c, cols],
-                            rhs=f_codes[k,][:, c, :].bitcast(E4M3),
-                            rhs_scale=f_sc[k,][:, c, :],
-                            start=(c == 0),
-                            stop=(c == C - 1),
-                        )
-
-        def out_rows(n, first, count):
-            i, ch = CHUNKS[n]
-            return out[i].rearrange("(p j) d -> p j d", j=J)[:, first : first + count, ch * P : (ch + 1) * P]
+        def synth(k, first, count, number):
+            bank = psum.tile([P, count, P * len(PIECES[k])], F32, tag="b%d" % number, name="o_ps")
+            o_ps[k, first] = bank
+            for r in range(count):
+                cols = slice((first + r) * P, (first + r + 1) * P)
+                for c in range(C):
+                    nc.tensor.matmul_mx(
+                        out=bank[:, r, :],
+                        lhsT=q_codes[:, c, cols].bitcast(E4M3),
+                        lhsT_scale=q_sc[:, c, cols],
+                        rhs=f_codes[k,][:, c, :].bitcast(E4M3),
+                        rhs_scale=f_sc[k,][:, c, :],
+                        start=(c == 0),
+                        stop=(c == C - 1),
+                    )
 
         def store(k, first, engine="scalar"):
             bank = o_ps[k, first]
-            count = bank.shape[1]
-            o_sb = outp.tile([P, count, P], F32)
+            count, width = bank.shape[1], bank.shape[2]
+            o_sb = outp.tile([P, count, width], F32)
             if engine == "vector":
                 nc.vector.tensor_copy(out=o_sb[:], in_=bank[:])
             else:
                 nc.scalar.copy(out=o_sb[:], in_=bank[:])
-            nc.sync.dma_start(out=out_rows(PIECES[k][0], first, count), in_=o_sb[:])
-
-        def store_pair(k, half):
-            o_two = outp.tile([P, B, 4, P], F32, bufs=3)
-            for r in range(2):
-                bank = o_ps[k, 4 * half + 2 * r]
-                nc.scalar.copy(
-                    out=o_two[:, :, 2 * r : 2 * r + 2, :], in_=bank[:].rearrange("p r (i d) -> p i r d", i=B)
-                )
-            for i in range(B):
-                nc.sync.dma_start(out=out_rows(PIECES[k][i], 4 * half, 4), in_=o_two[:, i, :, :])
-
-        def store_piece(k):
-            for first, _, _ in OUT_BANKS[k]:
-                store(k, first)
+            i, ch = CHUNKS[PIECES[k][0]]
+            rows = out[i].rearrange("(p j) d -> p j d", j=J)[:, first : first + count, ch * P : ch * P + width]
+            nc.sync.dma_start(out=rows, in_=o_sb[:])
 
         nc.sync.dma_start(out=rhs_rows[63:64, :], in_=om.rearrange("(o m) -> o m", o=1))
         nc.sync.dma_start(out=lhs_rows[127:128, :], in_=nu.rearrange("(o n) -> o n", o=1))
@@ -413,119 +395,141 @@ def tile_cauchytransferfunctionfilter_w4_kernel(
         load_x(1, 0)
         load_x(1, 1)
         load_q(0, 1)
+        load_q(1, 1)
         nc.sync.dma_start(out=c_raw[:], in_=c_words[0])
         load_c_scales()
-        load_q(1, 1)
 
         both, first_pass, second_pass = slice(0, G), slice(0, 1), slice(1, G)
+        left, right = slice(0, P), slice(P, H)
         q_banks = [(c, hs, jj) for hs in range(2) for c in range(C) for jj in range(2)]
         for tm in range(T):
             make_de(tm)
-        for bank in q_banks[:4]:
-            turn_q(*bank)
-        widen_x(UNITS[2], 0, "scalar", range(1))
+        for bank, number in zip(q_banks[:4], (4, 5, 6, 7)):
+            turn_q(*bank, number)
+        widen_x(2, 0, "scalar", range(1))
         for pair in ((0, 1), (2, 3)):
             for tm in pair:
                 square(tm)
             for tm in pair:
                 make_root(tm)
-        widen_x(UNITS[2], 0, "scalar", range(1, 2))
         for g in range(G):
-            widen_x(UNITS[1], g, "scalar")
-        for g in range(G):
-            widen_x(UNITS[0], g, "vector")
+            widen_x(0, g, "vector")
         for g in range(G):
             permute_p(g)
-        interleave_x(0, both, "vector")
-        interleave_x(2, both, "vector")
+        interleave_x(0, both, left, "vector")
+        interleave_x(0, both, right, "vector")
         quant_x(0)
         make_w(0)
         permute_p_scales()
-        make_gr(0, "gpsimd")
-        make_gi(0)
-        make_gi(1)
-        make_gr(1, "scalar")
-        make_u(0)
         make_w(1)
-        quant_x(2)
-        make_u(2)
-        make_gr(2, "gpsimd")
-        make_gi(2)
-        make_gi(3)
-        for bank in q_banks[:2]:
-            drain_q(*bank)
-        make_gr(3, "scalar")
-        for bank in q_banks[2:4]:
-            drain_q(*bank)
-        for bank in q_banks[4:6]:
-            turn_q(*bank)
-        drain_u(0)
-        drain_u(2)
-
-        interleave_x(1, both, "vector")
-        quant_g("i")
-        make_k(0, "i")
+        make_gr(0, 3, "gpsimd")
         quant_x(1)
-        make_u(1)
-        quant_g("r")
-        make_k(0, "r")
-        drain_u(1)
-        for bank in q_banks[4:6]:
+        for tm in range(T):
+            make_gi(tm)
+        for bank in q_banks[:4]:
             drain_q(*bank)
-        for bank in q_banks[6:]:
-            turn_q(*bank)
-            drain_q(*bank)
-        make_k(1)
+        make_gr(3, 1, "scalar")
+        make_u(0, 4)
+        for bank, number in zip(q_banks[4:6], (5, 6)):
+            turn_q(*bank, number)
+        make_u(1, 7)
         quant_q(0, 0)
-        interleave_x(3, both, "gpsimd", "q_0_0")
+        quant_g("i")
+        make_k(0, "i", 2)
+        quant_g("r")
+        make_k(0, "r", 3)
+        widen_x(1, 0, "scalar")
+        widen_x(1, 1, "scalar")
+        drain_u(0)
+        drain_u(1)
+        make_k(1, "i", 4)
+        make_k(1, "r", 7)
+        for bank, number in zip(q_banks[6:], (0, 1)):
+            turn_q(*bank, number)
+        interleave_x(1, both, slice(0, 192), "gpsimd", "g_r")
         quant_q(1, 0)
         make_f(0)
         make_f(1)
-        make_k(2, "i")
-        quant_x(3)
-        make_u(3)
+        for bank in q_banks[4:6]:
+            drain_q(*bank)
+        widen_x(2, 0, "scalar", range(1, 3))
+        make_k(2, "i", 5)
+        make_k(2, "r", 6)
+        for bank in q_banks[6:]:
+            drain_q(*bank)
+        drain_k(2)
+        quant_x(2)
+        make_u(2, 0)
+        interleave_x(1, both, slice(192, H), "vector")
         quant_f(0)
-        quant_q(0, 1)
-        quant_q(1, 1)
-        widen_x(UNITS[2], 0, "scalar", range(2, T))
-        drain_k(2, "i")
+        quant_x(3)
+        synth(0, 0, 2, 5)
+        make_u(3, 1)
+        synth(0, 2, 2, 6)
+        drain_u(2)
+        widen_x(2, 0, "scalar", range(3, T))
+        store(0, 0)
         drain_u(3)
-        synth(0, slice(0, 2))
-        make_k(2, "r")
-        synth(0, slice(2, 4))
-        widen_x(UNITS[2], 1, "vector")
-        store_pair(0, 0)
-        drain_k(2, "r")
-        make_k(3, "i")
-        widen_x(UNITS[3], 0, "scalar")
-        store_pair(0, 1)
-        widen_x(UNITS[3], 1, "scalar", range(LAST_PASS_ON_SCALAR))
-
-        last = len(CHUNKS) - 1
-        for n in range(2, last):
-            if n > 2:
-                quant_f(n - 2)
-                synth(n - 2)
-            if n == 4:
-                drain_k(3)
-            if n + 2 <= last:
-                interleave_x(n + 2, first_pass, "vector")
-                interleave_x(n + 2, second_pass, "gpsimd", "f_%d" % (n - 2) if n > 2 else "q_1_1")
-            make_f(n)
-            if n == 3:
-                make_k(3, "r")
-            if n + 2 <= last:
-                quant_x(n + 2)
-                make_u(n + 2)
-            if n == 2:
-                widen_x(UNITS[3], 1, "vector", range(LAST_PASS_ON_SCALAR, T))
-            if n > 2:
-                store_piece(n - 2)
-        quant_f_in_parts(last - 2)
-        synth(last - 2)
-        store_piece(last - 2)
-        make_f(last)
-        quant_f_in_parts(last - 1)
-        synth(last - 1)
-        for place, (first, _, _) in enumerate(OUT_BANKS[last - 1]):
-            store(last - 1, first, "vector" if place % 2 else "scalar")
+        quant_q(0, 1)
+        widen_x(2, 1, "vector")
+        quant_q(1, 1)
+        synth(0, 4, 2, 0)
+        synth(0, 6, 2, 1)
+        store(0, 2)
+        interleave_x(2, second_pass, left, "gpsimd", "q_1_1")
+        interleave_x(2, first_pass, left, "vector")
+        make_f(2)
+        make_k(3, "i", 2)
+        make_k(3, "r", 3)
+        quant_x(4)
+        make_u(4, 5)
+        quant_f(1)
+        widen_x(3, 0, "scalar")
+        widen_x(3, 1, "scalar")
+        store(0, 4)
+        store(0, 6)
+        synth(1, 0, 4, 6)
+        interleave_x(2, second_pass, right, "gpsimd", "f_1")
+        interleave_x(2, first_pass, right, "vector")
+        make_f(3)
+        synth(1, 4, 4, 4)
+        quant_x(5)
+        make_u(5, 7)
+        quant_f(2)
+        store(1, 0)
+        drain_k(3, "i")
+        store(1, 4)
+        drain_k(3, "r")
+        synth(2, 0, 4, 0)
+        synth(2, 4, 4, 1)
+        interleave_x(3, second_pass, left, "gpsimd", "f_2")
+        interleave_x(3, first_pass, left, "vector")
+        make_f(4)
+        quant_x(6)
+        make_u(6, 5)
+        quant_f(3)
+        store(2, 0)
+        store(2, 4)
+        synth(3, 0, 4, 2)
+        synth(3, 4, 4, 3)
+        interleave_x(3, second_pass, right, "gpsimd", "f_3")
+        interleave_x(3, first_pass, right, "vector")
+        make_f(5)
+        quant_x(7)
+        make_u(7, 7)
+        quant_f(4)
+        store(3, 0)
+        store(3, 4)
+        for first, number in zip(range(0, J, 2), (6, 4, 0, 1)):
+            synth(4, first, 2, number)
+            store(4, first)
+        make_f(6)
+        quant_f_in_parts(5)
+        for first, count, number in ((0, 2, 2), (2, 3, 3), (5, 3, 5)):
+            synth(5, first, count, number)
+            store(5, first)
+        make_f(7)
+        quant_f_in_parts(6)
+        for first, number in zip(range(0, J, 2), (6, 4, 0, 1)):
+            synth(6, first, 2, number)
+            store(6, first, "vector" if first % 4 else "scalar")

@@ -46,7 +46,7 @@ def tile_cauchytransferfunctionfilter_w4_kernel(
         def tiles(name, keys, shape, dtype):
             made = {}
             for key in keys:
-                one = keep.tile(shape, dtype, name=name + "_" + "_".join(str(v) for v in key), align_bytes=64)
+                one = keep.tile(shape, dtype, name=name + "_" + "_".join(str(v) for v in key), align_bytes=256)
                 made[key] = one
             return made
 
@@ -57,27 +57,27 @@ def tile_cauchytransferfunctionfilter_w4_kernel(
         ident = keep.tile([P, P], F32)
         b_col = keep.tile([P, T], BF16)
         xs = keep.tile([P, G, T], F32)
-        p_raw = keep.tile([P, G, 2 * M], U8, align_bytes=64)
-        p_scale_raw = keep.tile([P, G, M], U8, align_bytes=64)
-        p_perm = keep.tile([P, G, 2 * M], U8, align_bytes=64)
-        p_scale = keep.tile([P, G, M], U8, align_bytes=64)
-        c_raw = keep.tile([P, 2 * D], U8, align_bytes=64)
-        c_scale = keep.tile([P, D], U8, align_bytes=64)
+        p_raw = keep.tile([P, G, 2 * M], U8, align_bytes=256)
+        p_scale_raw = keep.tile([P, G, M], U8, align_bytes=256)
+        p_perm = keep.tile([P, G, 2 * M], U8, align_bytes=256)
+        p_scale = keep.tile([P, G, M], U8, align_bytes=256)
+        c_raw = keep.tile([P, 2 * D], U8, align_bytes=256)
+        c_scale = keep.tile([P, D], U8, align_bytes=256)
         x_raw = tiles("x_raw", [(i, g) for i in range(B) for g in range(G)], [P, T * D], U8)
         q_raw = tiles("q_raw", [(c, hs) for c in range(C) for hs in range(2)], [P, J // 2, M], BF16)
         q_bf = {}
         for c in range(C):
             for hs in range(2):
-                q_words = stage.tile([P, S // 2, T], BF16, tag="q_%d_%d" % (c, hs), name="q_bf", align_bytes=64)
+                q_words = stage.tile([P, S // 2, T], BF16, tag="q_%d_%d" % (c, hs), name="q_bf", align_bytes=256)
                 q_bf[c, hs] = q_words
-        q_codes = keep.tile([P, C, S], U32, align_bytes=64)
-        q_sc = keep.tile([P, C, S], U8, align_bytes=64)
+        q_codes = keep.tile([P, C, S], U32, align_bytes=256)
+        q_sc = keep.tile([P, C, S], U8, align_bytes=256)
         root = keep.tile([P, T, M], F32)
         w = keep.tile([P, T, M], F32)
         parts = [("r",), ("i",)]
         g_bf = {}
         for key in parts:
-            g_words = stage.tile([P, M, T], BF16, tag="g_" + key[0], name="g_bf", align_bytes=64)
+            g_words = stage.tile([P, M, T], BF16, tag="g_" + key[0], name="g_bf", align_bytes=256)
             g_bf[key] = g_words
         g_codes = tiles("g_codes", parts, [P, M], U32)
         g_sc = tiles("g_sc", parts, [P, M], U8)
@@ -90,7 +90,7 @@ def tile_cauchytransferfunctionfilter_w4_kernel(
         f_bf, f_codes, f_sc = {}, {}, {}
         for k, piece in enumerate(PIECES):
             width = P * len(piece)
-            f_words = stage.tile([P, 2, width, T], BF16, tag="f_%d" % k, name="f_bf", align_bytes=64)
+            f_words = stage.tile([P, 2, width, T], BF16, tag="f_%d" % k, name="f_bf", align_bytes=256)
             f_bf[k,] = f_words
             f_codes.update(tiles("f_codes", [(k,)], [P, 2, width], U32))
             f_sc.update(tiles("f_sc", [(k,)], [P, 2, width], U8))
@@ -207,7 +207,7 @@ def tile_cauchytransferfunctionfilter_w4_kernel(
             if spent is None:
                 spent = "x_%d_%d_%d" % (unit, passes.start, cols.start)
             shape = [P, passes.stop - passes.start, cols.stop - cols.start, T]
-            dst = stage.tile(shape, BF16, tag=spent, name="inter", align_bytes=64)
+            dst = stage.tile(shape, BF16, tag=spent, name="inter", align_bytes=256)
             for e in range(2):
                 lo, hi = max(cols.start, P * e), min(cols.stop, P * (e + 1))
                 if lo < hi:

@@ -154,8 +154,7 @@ def tile_cauchytransferfunctionfilter_w4_kernel(
         def out_runs(words):
             return words.rearrange("p (c e) t -> p c t e", e=4)
 
-        def make_gr(first, count, engine):
-            cols = slice(P * first, P * (first + count))
+        def make_gr(cols, engine):
             dst, src = g_bf["r",][:, cols, :], w[:, :, cols]
             if engine == "scalar":
                 nc.scalar.activation(out=out_runs(dst), in_=in_runs(src), func=ACT.Copy, scale=0.5)
@@ -422,13 +421,13 @@ def tile_cauchytransferfunctionfilter_w4_kernel(
         make_w(0)
         permute_p_scales()
         make_w(1)
-        make_gr(0, 3, "gpsimd")
+        make_gr(slice(0, 320), "gpsimd")
         quant_x(1)
         for tm in range(T):
             make_gi(tm)
         for bank in q_banks[:4]:
             drain_q(*bank)
-        make_gr(3, 1, "scalar")
+        make_gr(slice(320, M), "scalar")
         make_u(0, 4)
         for bank, number in zip(q_banks[4:6], (5, 6)):
             turn_q(*bank, number)
@@ -498,8 +497,8 @@ def tile_cauchytransferfunctionfilter_w4_kernel(
         quant_f(2)
         store(1, 0)
         drain_k(3, "i")
-        store(1, 4)
         drain_k(3, "r")
+        store(1, 4)
         synth(2, 0, 4, 0)
         synth(2, 4, 4, 1)
         interleave_x(3, second_pass, left, "gpsimd", "f_2")

@@ -230,7 +230,7 @@ def tile_cauchytransferfunctionfilter_w4_kernel(
 
         def quant_x(n):
             chunk = CHUNKS[n]
-            for passes, cols, words, whole in inter[n]:
+            for passes, cols, words, whole in reversed(inter[n]):
                 if whole:
                     nc.vector.quantize_mx(
                         out=x_codes[chunk][:, passes, :].rearrange("p g d -> p (g d)").bitcast(E4M3),
@@ -457,9 +457,9 @@ def tile_cauchytransferfunctionfilter_w4_kernel(
         for bank in q_banks[6:]:
             drain_q(*bank)
         drain_k(2)
+        interleave_x(1, both, slice(192, H), "vector")
         quant_x(2)
         make_u(2, 0)
-        interleave_x(1, both, slice(192, H), "vector")
         quant_f(0)
         quant_x(3)
         synth(0, 0, 2, 5)

@@ -519,16 +519,16 @@ def tile_cauchytransferfunctionfilter_w4_kernel(
         quant_f(4)
         store(3, 0)
         store(3, 4)
-        for first, number in zip(range(0, J, 2), (6, 4, 0, 1)):
-            synth(4, first, 2, number)
+        for place, (first, count, number) in enumerate(((0, 3, 6), (3, 3, 4), (6, 2, 0))):
+            synth(4, first, count, number)
             store(4, first)
         make_f(6)
         quant_f_in_parts(5)
-        for first, count, number in ((0, 2, 2), (2, 3, 3), (5, 3, 5)):
+        for place, (first, count, number) in enumerate(((0, 3, 2), (3, 3, 3), (6, 2, 5))):
             synth(5, first, count, number)
             store(5, first)
         make_f(7)
         quant_f_in_parts(6)
-        for first, number in zip(range(0, J, 2), (6, 4, 0, 1)):
-            synth(6, first, 2, number)
-            store(6, first, "vector" if first % 4 else "scalar")
+        for place, (first, count, number) in enumerate(((0, 3, 1), (3, 3, 6), (6, 2, 4))):
+            synth(6, first, count, number)
+            store(6, first, "vector" if place % 2 else "scalar")

from contextlib import ExitStack

import concourse.mybir as mybir
from concourse.masks import make_identity

B, S, D, M, N, C = 2, 1024, 512, 512, 512, 2
FLOPS = 2 * (2 * M * N * D + B * M * S * D + 2 * B * S * M * D)

F32 = mybir.dt.float32
BF16 = mybir.dt.bfloat16
U32 = mybir.dt.uint32
I32 = mybir.dt.int32
U16 = mybir.dt.uint16
U8 = mybir.dt.uint8
F8 = mybir.dt.float8_e4m3fn
E4M3 = mybir.dt.float8_e4m3fn_x4
E2M1 = mybir.dt.float4_e2m1fn_x4
ALU = mybir.AluOpType
ACT = mybir.ActivationFunctionType

ONE_TWICE = 0x3F803F80
MINUS_ONE_TWICE = 0xBF80BF80

P = 128
T = 4
G = S // (P * T)
J = S // P
H = 256
UNITS = [(0, 0), (1, 0), (0, 1), (1, 1)]
CHUNKS = [(i, 2 * h + e) for i, h in UNITS for e in range(2)]
U_COPIED = [0, 1, 2, 3]
PIECES = [[0, 1], [2], [3], [4], [5], [6], [7]]


def tile_cauchytransferfunctionfilter_w4_kernel(
    tc, x_bytes, x_scale, p_words, p_scales, om, nu, b, c_words, c_scales, q, out
):
    nc = tc.nc
    with ExitStack() as ctx:
        keep = ctx.enter_context(tc.tile_pool(name="keep", bufs=1))
        stage = ctx.enter_context(tc.tile_pool(name="stage", bufs=1))
        outp = ctx.enter_context(tc.tile_pool(name="outp", bufs=12))
        psum = ctx.enter_context(tc.psum_pool(name="psum", bufs=1))
        ctx.enter_context(tc.manual_schedule())

        def tiles(name, keys, shape, dtype):
            made = {}
            for key in keys:
                one = keep.tile(shape, dtype, name=name + "_" + "_".join(str(v) for v in key), align_bytes=256)
                made[key] = one
            return made

        lhs_rows = keep.tile([P, N], BF16)
        rhs_rows = keep.tile([P, M], BF16)
        quarter = keep.tile([P, 1], F32)
        warm = keep.tile([P, 1], F32)
        ident = keep.tile([P, P], F32)
        b_col = keep.tile([P, T], BF16)
        xs = keep.tile([P, G, T], F32)
        p_raw = keep.tile([P, G, 2 * M], U8, align_bytes=256)
        p_scale_raw = keep.tile([P, G, M], U8, align_bytes=256)
        p_perm = keep.tile([P, G, 2 * M], U8, align_bytes=256)
        p_scale = keep.tile([P, G, M], U8, align_bytes=256)
        c_raw = keep.tile([P, 2 * D], U8, align_bytes=256)
        c_scale = keep.tile([P, D], U8, align_bytes=256)
        x_raw = tiles("x_raw", [(i, g) for i in range(B) for g in range(G)], [P, T * D], U8)
        q_raw = tiles("q_raw", [(c, hs) for c in range(C) for hs in range(2)], [P, J // 2, M], BF16)
        q_bf = {}
        for c in range(C):
            for hs in range(2):
                q_words = stage.tile([P, S // 2, T], BF16, tag="q_%d_%d" % (c, hs), name="q_bf", align_bytes=256)
                q_bf[c, hs] = q_words
        q_codes = keep.tile([P, C, S], U32, align_bytes=256)
        q_sc = keep.tile([P, C, S], U8, align_bytes=256)
        root = keep.tile([P, T, M], F32)
        w = keep.tile([P, T, M], F32)
        parts = [("r",), ("i",)]
        g_bf = {}
        for key in parts:
            g_words = stage.tile([P, M, T], BF16, tag="g_" + key[0], name="g_bf", align_bytes=256)
            g_bf[key] = g_words
        g_codes = tiles("g_codes", parts, [P, M], U32)
        g_sc = tiles("g_sc", parts, [P, M], U8)
        u_sb = tiles("u_sb", [CHUNKS[n] for n in U_COPIED], [P, P, T], F32)
        k_sb = tiles("k_sb", [(2,), (3,)], [P, 2, P, T], F32)
        wide = tiles("wide", UNITS, [P, G, T, H], BF16)
        inter = {}
        x_codes = tiles("x_codes", CHUNKS, [P, G, P], U32)
        x_sc = tiles("x_sc", CHUNKS, [P, G, P], U8)
        f_bf, f_codes, f_sc = {}, {}, {}
        for k, piece in enumerate(PIECES):
            width = P * len(piece)
            f_words = stage.tile([P, 2, width, T], BF16, tag="f_%d" % k, name="f_bf", align_bytes=256)
            f_bf[k,] = f_words
            f_codes.update(tiles("f_codes", [(k,)], [P, 2, width], U32))
            f_sc.update(tiles("f_sc", [(k,)], [P, 2, width], U8))
        de_ps, q_ps, k_ps, u_ps, o_ps = {}, {}, {}, {}, {}

        def load_x(i, g, slots=slice(0, T)):
            rows = x_bytes[i, g * P * T : (g + 1) * P * T, :].rearrange("(p t) d -> p (t d)", t=T)
            cols = slice(slots.start * D, slots.stop * D)
            nc.sync.dma_start(out=x_raw[i, g][:, cols], in_=rows[:, cols])

        def load_q(c, hs):
            rows = q[c].rearrange("(p j) m -> p j m", j=J)[:, 4 * hs : 4 * hs + 4, :]
            nc.sync.dma_start(out=q_raw[c, hs][:], in_=rows)

        def load_p_scales():
            for quad in range(4):
                nc.sync.dma_start(
                    out=p_scale_raw[32 * quad : 32 * quad + 4, :, :].bitcast(I32),
                    in_=p_scales[:, 4 * quad : 4 * quad + 4, :].rearrange("g r m -> r g m").bitcast(I32),
                )

        def load_c_scales():
            for quad in range(4):
                nc.sync.dma_start(
                    out=c_scale[32 * quad : 32 * quad + 4, :].bitcast(I32),
                    in_=c_scales[0, 4 * quad : 4 * quad + 4, :].bitcast(I32),
                )

        def make_de(tm):
            bank = psum.tile([P, T, P], F32, tag="b%d" % tm, name="de_ps")
            de_ps[tm] = bank
            for t in range(T):
                nc.tensor.matmul(
                    out=bank[:, t, :], lhsT=lhs_rows[:, t::T], rhs=rhs_rows[:, tm::T], start=True, stop=True
                )

        def square(tm):
            nc.scalar.activation(out=root[:, :, P * tm : P * (tm + 1)], in_=de_ps[tm][:], func=ACT.Square)

        def make_root(tm):
            cols = slice(P * tm, P * (tm + 1))
            nc.scalar.activation(
                out=root[:, :, cols], in_=root[:, :, cols], func=ACT.Abs_reciprocal_sqrt, bias=quarter[:], scale=1.0
            )

        def make_w(hm):
            cols = slice(256 * hm, 256 * (hm + 1))
            for t in range(T):
                nc.vector.scalar_tensor_tensor(
                    out=w[:, t, cols],
                    in0=root[:, t, cols],
                    scalar=b_col[:, t : t + 1],
                    in1=root[:, t, cols],
                    op0=ALU.mult,
                    op1=ALU.mult,
                )

        def in_runs(planes):
            return planes.rearrange("p t (c e) -> p c t e", e=4)

        def out_runs(words):
            return words.rearrange("p (c e) t -> p c t e", e=4)

        def make_gr(cols, engine):
            dst, src = g_bf["r",][:, cols, :], w[:, :, cols]
            if engine == "scalar":
                nc.scalar.activation(out=out_runs(dst), in_=in_runs(src), func=ACT.Copy, scale=0.5)
            else:
                src = src.rearrange("p t m -> p m t")
                nc.gpsimd.tensor_scalar(out=dst, in0=src, scalar1=0.5, scalar2=0.0, op0=ALU.mult, op1=ALU.add)

        def make_gi(tm):
            cols = slice(P * tm, P * (tm + 1))
            nc.vector.tensor_tensor(
                out=out_runs(g_bf["i",][:, cols, :]),
                in0=in_runs(de_ps[tm][:]),
                in1=in_runs(w[:, :, cols]),
                op=ALU.mult,
            )

        def quant_g(part):
            nc.vector.quantize_mx(
                out=g_codes[part,][:].bitcast(E4M3),
                scales=g_sc[part,][:],
                in_=g_bf[part,][:].rearrange("p m t -> p (m t)"),
            )

        def permute_p(g):
            nc.vector.tensor_copy(
                out=p_perm[:, g, :].bitcast(U16).rearrange("p (t m) -> p t m", t=T),
                in_=p_raw[:, g, :].bitcast(U16).rearrange("p (m t) -> p t m", t=T),
            )

        def permute_p_scales():
            nc.vector.tensor_copy(
                out=p_scale[:].rearrange("p g (t m) -> p g t m", t=T),
                in_=p_scale_raw[:].rearrange("p g (m t) -> p g t m", t=T),
            )

        def widen_x(unit, g, engine, slots=range(T), cols=slice(0, H)):
            i, h = UNITS[unit]
            for t in slots:
                src = x_raw[i, g][:, t * D + h * H + cols.start : t * D + h * H + cols.stop].bitcast(F8)
                scale = xs[:, g, t : t + 1]
                dst = wide[i, h][:, g, t, cols]
                if engine == "vector":
                    nc.vector.tensor_scalar(out=dst, in0=src, scalar1=scale, scalar2=None, op0=ALU.mult)
                else:
                    nc.scalar.activation(out=dst, in_=src, func=ACT.Copy, scale=scale)

        def interleave_x(unit, passes, cols, engine, spent=None):
            src = wide[UNITS[unit]][:, passes, :, cols]
            if spent is None:
                spent = "x_%d_%d_%d" % (unit, passes.start, cols.start)
            shape = [P, passes.stop - passes.start, cols.stop - cols.start, T]
            dst = stage.tile(shape, BF16, tag=spent, name="inter", align_bytes=256)
            for e in range(2):
                lo, hi = max(cols.start, P * e), min(cols.stop, P * (e + 1))
                if lo < hi:
                    part = dst[:, :, lo - cols.start : hi - cols.start, :]
                    whole = hi - lo == P and shape[2] == P
                    inter.setdefault(2 * unit + e, []).append((passes, slice(lo - P * e, hi - P * e), part, whole))
            if engine == "gpsimd":
                nc.gpsimd.tensor_scalar(
                    out=dst[:],
                    in0=src.rearrange("p g t d -> p g d t"),
                    scalar1=1.0,
                    scalar2=0.0,
                    op0=ALU.mult,
                    op1=ALU.add,
                )
            else:
                nc.vector.tensor_copy(
                    out=dst[:].rearrange("p g (c e) t -> p g c t e", e=4),
                    in_=src.rearrange("p g t (c e) -> p g c t e", e=4),
                )

        def quant_x(n):
            chunk = CHUNKS[n]
            for passes, cols, words, whole in reversed(inter[n]):
                if whole:
                    nc.vector.quantize_mx(
                        out=x_codes[chunk][:, passes, :].rearrange("p g d -> p (g d)").bitcast(E4M3),
                        scales=x_sc[chunk][:, passes, :].rearrange("p g d -> p (g d)"),
                        in_=words.rearrange("p g d t -> p (g d t)"),
                    )
                else:
                    for g in range(passes.start, passes.stop):
                        nc.vector.quantize_mx(
                            out=x_codes[chunk][:, g, cols].bitcast(E4M3),
                            scales=x_sc[chunk][:, g, cols],
                            in_=words[:, g - passes.start, :, :].rearrange("p d t -> p (d t)"),
                        )

        def turn_q(c, hs, jj, number):
            bank = psum.tile([P, 2, 2, P], F32, tag="b%d" % number, name="q_ps")
            q_ps[c, hs, jj] = bank
            words = q_raw[c, hs][:].rearrange("p j m -> p (j m)").bitcast(F32)
            for k in range(2):
                base = (2 * jj + k) * (M // 2)
                for u in range(2):
                    nc.tensor.transpose(bank[:, k, u, :], words[:, base + u : base + M // 2 : 2], ident[:])

        def drain_q(c, hs, jj):
            nc.scalar.copy(
                out=q_bf[c, hs][:, 2 * jj * P : (2 * jj + 2) * P, :]
                .rearrange("p s t -> p (s t)")
                .bitcast(F32)
                .rearrange("p (k s u) -> p k s u", k=2, u=2),
                in_=q_ps[c, hs, jj][:].rearrange("p k u s -> p k s u"),
            )

        def quant_q(c, hs):
            rows = slice(hs * S // 2, (hs + 1) * S // 2)
            nc.vector.quantize_mx(
                out=q_codes[:, c, rows].bitcast(E4M3),
                scales=q_sc[:, c, rows],
                in_=q_bf[c, hs][:].rearrange("p s t -> p (s t)"),
            )

        def make_k(ch, part, number):
            if True:
                bank = psum.tile([P, T, P], F32, tag="b%d" % number, name="k_ps")
                k_ps[part, ch] = bank
                for t in range(T):
                    cols = slice(t * P, (t + 1) * P)
                    nc.tensor.matmul_mx(
                        out=bank[:, t, :],
                        lhsT=g_codes[part,][:, cols].bitcast(E4M3),
                        lhsT_scale=g_sc[part,][:, cols],
                        rhs=c_raw[:, 2 * P * ch : 2 * P * (ch + 1)].bitcast(E2M1),
                        rhs_scale=c_scale[:, P * ch : P * (ch + 1)],
                        start=True,
                        stop=True,
                    )

        def drain_k(ch, parts="ir"):
            for part in parts:
                nc.scalar.copy(
                    out=k_sb[ch,][:, "ri".index(part), :, :], in_=k_ps[part, ch][:].rearrange("p t d -> p d t")
                )

        def make_u(n, number):
            chunk = CHUNKS[n]
            bank = psum.tile([P, T, P], F32, tag="b%d" % number, name="u_ps")
            u_ps[n] = bank
            for t in range(T):
                for g in range(G):
                    nc.tensor.matmul_mx(
                        out=bank[:, t, :],
                        lhsT=p_perm[:, g, 2 * P * t : 2 * P * (t + 1)].bitcast(E2M1),
                        lhsT_scale=p_scale[:, g, P * t : P * (t + 1)],
                        rhs=x_codes[chunk][:, g, :].bitcast(E4M3),
                        rhs_scale=x_sc[chunk][:, g, :],
                        start=(g == 0),
                        stop=(g == G - 1),
                    )

        def drain_u(n):
            nc.scalar.copy(out=u_sb[CHUNKS[n]][:], in_=u_ps[n][:].rearrange("p t d -> p d t"))

        piece_of = {n: (k, piece.index(n)) for k, piece in enumerate(PIECES) for n in piece}

        def make_f(n):
            k, place = piece_of[n]
            ch = CHUNKS[n][1]
            for c, part in ((1, "i"), (0, "r")):
                if CHUNKS[n] in u_sb:
                    in_psum, in_sbuf = k_ps[part, ch], u_sb[CHUNKS[n]][:]
                else:
                    in_psum, in_sbuf = u_ps[n], k_sb[ch,][:, c, :, :]
                nc.vector.tensor_tensor(
                    out=f_bf[k,][:, c, P * place : P * (place + 1), :],
                    in0=in_psum[:].rearrange("p t d -> p d t"),
                    in1=in_sbuf,
                    op=ALU.mult,
                )

        def quant_f(k, parts=slice(0, 2)):
            nc.vector.quantize_mx(
                out=f_codes[k,][:, parts, :].rearrange("p k d -> p (k d)").bitcast(E4M3),
                scales=f_sc[k,][:, parts, :].rearrange("p k d -> p (k d)"),
                in_=f_bf[k,][:, parts, :, :].rearrange("p k d t -> p (k d t)"),
            )

        def quant_f_in_parts(k):
            quant_f(k, slice(1, 2))
            quant_f(k, slice(0, 1))

        def synth(k, first, count, number):
            bank = psum.tile([P, count, P * len(PIECES[k])], F32, tag="b%d" % number, name="o_ps")
            o_ps[k, first] = bank
            for r in range(count):
                cols = slice((first + r) * P, (first + r + 1) * P)
                for c in range(C):
                    nc.tensor.matmul_mx(
                        out=bank[:, r, :],
                        lhsT=q_codes[:, c, cols].bitcast(E4M3),
                        lhsT_scale=q_sc[:, c, cols],
                        rhs=f_codes[k,][:, c, :].bitcast(E4M3),
                        rhs_scale=f_sc[k,][:, c, :],
                        start=(c == 0),
                        stop=(c == C - 1),
                    )

        def store(k, first, engine="scalar"):
            bank = o_ps[k, first]
            count, width = bank.shape[1], bank.shape[2]
            o_sb = outp.tile([P, count, width], F32)
            if engine == "vector":
                nc.vector.tensor_copy(out=o_sb[:], in_=bank[:])
            else:
                nc.scalar.copy(out=o_sb[:], in_=bank[:])
            i, ch = CHUNKS[PIECES[k][0]]
            rows = out[i].rearrange("(p j) d -> p j d", j=J)[:, first : first + count, ch * P : ch * P + width]
            nc.sync.dma_start(out=rows, in_=o_sb[:])

        nc.sync.dma_start(out=rhs_rows[63:64, :], in_=om.rearrange("(o m) -> o m", o=1))
        nc.sync.dma_start(out=lhs_rows[127:128, :], in_=nu.rearrange("(o n) -> o n", o=1))
        nc.sync.dma_start(out=xs[:], in_=x_scale.rearrange("o (g p t) w -> p (o g) (t w)", p=P, t=T))
        for g in range(G):
            load_x(0, g, slice(0, 2))
            load_x(0, g, slice(2, T))
        for g in range(G):
            nc.sync.dma_start(out=p_raw[:, g, :], in_=p_words[g])
        nc.sync.dma_start(out=b_col[:], in_=b.rearrange("(p t) -> p t", t=T))
        load_q(0, 0)

        make_identity(nc, ident[:])
        nc.vector.memset(quarter[:], 0.25)
        nc.scalar.activation(out=warm[:], in_=quarter[:], func=ACT.Abs_reciprocal_sqrt, bias=quarter[:], scale=1.0)
        nc.vector.memset(lhs_rows[0:64, :].bitcast(U32), ONE_TWICE)
        nc.vector.memset(rhs_rows[64:128, :].bitcast(U32), MINUS_ONE_TWICE)
        nc.vector.memset(rhs_rows[0:63, :].bitcast(F32), 0.0)
        nc.vector.memset(lhs_rows[64:127, :].bitcast(F32), 0.0)
        nc.vector.memset(p_scale_raw[:].rearrange("p g m -> p (g m)").bitcast(I32), 0)
        nc.vector.memset(c_scale[:].bitcast(I32), 0)

        load_p_scales()
        load_q(1, 0)
        load_x(1, 0)
        load_x(1, 1)
        load_q(0, 1)
        load_q(1, 1)
        nc.sync.dma_start(out=c_raw[:], in_=c_words[0])
        load_c_scales()

        both, first_pass, second_pass = slice(0, G), slice(0, 1), slice(1, G)
        left, right = slice(0, P), slice(P, H)
        q_banks = [(c, hs, jj) for hs in range(2) for c in range(C) for jj in range(2)]
        for tm in range(T):
            make_de(tm)
        for bank, number in zip(q_banks[:4], (4, 5, 6, 7)):
            turn_q(*bank, number)
        widen_x(2, 0, "scalar", range(1))
        for pair in ((0, 1), (2, 3)):
            for tm in pair:
                square(tm)
            for tm in pair:
                make_root(tm)
        for g in range(G):
            widen_x(0, g, "vector")
        for g in range(G):
            permute_p(g)
        interleave_x(0, both, left, "vector")
        interleave_x(0, both, right, "vector")
        quant_x(0)
        make_w(0)
        permute_p_scales()
        make_w(1)
        make_gr(slice(0, 320), "gpsimd")
        quant_x(1)
        for tm in range(T):
            make_gi(tm)
        for bank in q_banks[:4]:
            drain_q(*bank)
        make_gr(slice(320, M), "scalar")
        make_u(0, 4)
        for bank, number in zip(q_banks[4:6], (5, 6)):
            turn_q(*bank, number)
        make_u(1, 7)
        quant_q(0, 0)
        quant_g("i")
        make_k(0, "i", 2)
        quant_g("r")
        make_k(0, "r", 3)
        widen_x(1, 0, "scalar")
        widen_x(1, 1, "scalar")
        drain_u(0)
        drain_u(1)
        make_k(1, "i", 4)
        make_k(1, "r", 7)
        for bank, number in zip(q_banks[6:], (0, 1)):
            turn_q(*bank, number)
        interleave_x(1, both, slice(0, 192), "gpsimd", "g_r")
        quant_q(1, 0)
        make_f(0)
        make_f(1)
        for bank in q_banks[4:6]:
            drain_q(*bank)
        widen_x(2, 0, "scalar", range(1, 3))
        make_k(2, "i", 5)
        make_k(2, "r", 6)
        for bank in q_banks[6:]:
            drain_q(*bank)
        drain_k(2)
        interleave_x(1, both, slice(192, H), "vector")
        quant_x(2)
        make_u(2, 0)
        quant_f(0)
        quant_x(3)
        synth(0, 0, 2, 5)
        make_u(3, 1)
        synth(0, 2, 2, 6)
        drain_u(2)
        widen_x(2, 0, "scalar", range(3, T))
        store(0, 0)
        drain_u(3)
        quant_q(0, 1)
        widen_x(2, 1, "vector")
        quant_q(1, 1)
        synth(0, 4, 2, 0)
        synth(0, 6, 2, 1)
        store(0, 2)
        interleave_x(2, second_pass, left, "gpsimd", "q_1_1")
        interleave_x(2, first_pass, left, "vector")
        make_f(2)
        make_k(3, "i", 2)
        make_k(3, "r", 3)
        quant_x(4)
        make_u(4, 5)
        quant_f(1)
        widen_x(3, 0, "scalar")
        widen_x(3, 1, "scalar")
        store(0, 4)
        store(0, 6)
        synth(1, 0, 4, 6)
        interleave_x(2, second_pass, right, "gpsimd", "f_1")
        interleave_x(2, first_pass, right, "vector")
        make_f(3)
        synth(1, 4, 4, 4)
        quant_x(5)
        make_u(5, 7)
        quant_f(2)
        store(1, 0)
        drain_k(3, "i")
        drain_k(3, "r")
        store(1, 4)
        synth(2, 0, 4, 0)
        synth(2, 4, 4, 1)
        interleave_x(3, second_pass, left, "gpsimd", "f_2")
        interleave_x(3, first_pass, left, "vector")
        make_f(4)
        quant_x(6)
        make_u(6, 5)
        quant_f(3)
        store(2, 0)
        store(2, 4)
        synth(3, 0, 4, 2)
        synth(3, 4, 4, 3)
        interleave_x(3, second_pass, right, "gpsimd", "f_3")
        interleave_x(3, first_pass, right, "vector")
        make_f(5)
        quant_x(7)
        make_u(7, 7)
        quant_f(4)
        store(3, 0)
        store(3, 4)
        for place, (first, count, number) in enumerate(((0, 3, 6), (3, 3, 4), (6, 2, 0))):
            synth(4, first, count, number)
            store(4, first)
        make_f(6)
        quant_f_in_parts(5)
        for place, (first, count, number) in enumerate(((0, 3, 2), (3, 3, 3), (6, 2, 5))):
            synth(5, first, count, number)
            store(5, first)
        make_f(7)
        quant_f_in_parts(6)
        for place, (first, count, number) in enumerate(((0, 3, 1), (3, 3, 6), (6, 2, 4))):
            synth(6, first, count, number)
            store(6, first, "vector" if place % 2 else "scalar")
